import numpy as np
import ml_dtypes


def mxq(x, axis, fmt="e4m3"):
    dtype, down = {"e4m3": (ml_dtypes.float8_e4m3fn, 7), "e5m2": (ml_dtypes.float8_e5m2, 14)}[fmt]
    v = np.moveaxis(np.asarray(x, np.float32).astype(ml_dtypes.bfloat16).astype(np.float64), axis, -1)
    blocks = v.reshape(v.shape[:-1] + (-1, 32))
    amax = np.abs(blocks).max(-1, keepdims=True)
    byte = np.maximum(np.where(amax > 0, np.frexp(amax)[1] - 1 + 127, 0) - down, 1)
    scale = np.exp2(byte - 127.0)
    codes = (blocks / scale).astype(np.float32).astype(dtype).astype(np.float64)
    return np.moveaxis((codes * scale).reshape(v.shape), -1, axis)


WIDE = False


def mx_kscale(k):
    if not WIDE:
        return np.ones(k)
    levels = np.array([10, -10, 5, -5, 0])
    if k % 512:
        return np.exp2(np.random.permutation(np.resize(levels, k // 32))).repeat(32)
    a = np.empty((k // 512, 16))
    for p in range(k // 512):
        a[p, :8] = np.random.permutation(np.resize(levels, 8))
        for g in range(8):
            far = levels[np.abs(levels - a[p, g]) >= 10]
            a[p, g + 8] = far[np.random.randint(len(far))]
    return np.exp2(a.ravel()).repeat(32)


def f64(x):
    return np.asarray(x).astype(np.float64)


def striped(idx):
    return np.tile(idx.reshape(-1, 16).T, (8, 1)).astype(np.uint16)


def unstriped(offs):
    return offs[:16].T.reshape(-1).astype(np.int64)


E2M1 = np.array([0.0, 0.5, 1.0, 1.5, 2.0, 3.0, 4.0, 6.0, -0.0, -0.5, -1.0, -1.5, -2.0, -3.0, -4.0, -6.0])


def pack_weight(w, fmt):
    k, n = w.shape
    w = f64(np.asarray(w, np.float32).astype(ml_dtypes.bfloat16)).reshape(k // 32, 32, n)
    amax = np.abs(w).max(1)
    if fmt == "e4m3":
        byte = np.frexp(amax)[1] - 1 + 127 - 7
    else:
        mant, ex = np.frexp(amax / 6.0)
        byte = np.where(mant > 0.5, ex, ex - 1) + 127
    byte = np.clip(np.where(amax > 0, byte, 1), 1, 254)
    scaled = (w * np.exp2(127.0 - byte)[:, None, :]).reshape(k, n).astype(np.float32)
    by_word = np.ascontiguousarray(scaled.reshape(k // 512, 128, 4, n).transpose(0, 1, 3, 2))
    if fmt == "e4m3":
        words = by_word.astype(ml_dtypes.float8_e4m3fn).view(np.uint8)
    else:
        c = by_word.astype(ml_dtypes.float4_e2m1fn).view(np.uint8) & 0xF
        words = (c[..., 0::2] | (c[..., 1::2] << 4)).reshape(k // 512, 128, 2 * n)
    return np.ascontiguousarray(words), np.ascontiguousarray(byte.astype(np.uint8).reshape(k // 512, 16, n))


def unpack_weight(words, scales, fmt):
    g, _, n = scales.shape
    words = np.ascontiguousarray(words).reshape(g, 128, n, -1)
    if fmt == "e4m3":
        vals = words.view(ml_dtypes.float8_e4m3fn).astype(np.float64)
    else:
        nib = np.empty((g, 128, n, 4), np.uint8)
        nib[..., 0::2] = words & 0xF
        nib[..., 1::2] = words >> 4
        vals = E2M1[nib]
    vals = vals * np.repeat(np.exp2(scales.astype(np.float64) - 127.0), 8, axis=1)[..., None]
    return vals.transpose(0, 1, 3, 2).reshape(g * 512, n)


def relu(v):
    return np.maximum(v, 0.0)


K, T, E, C, H, N = 1024, 1024, 8, 128, 512, 256


def by_expert(wq, xq):
    return np.concatenate([wq[e].T @ xq[:, e * C:(e + 1) * C] for e in range(E)], axis=1)


def setup_inputs():
    n = np.random.standard_normal
    s = mx_kscale(K)[:, None]
    u = mx_kscale(H)
    w1 = [pack_weight(m, "e2m1") for m in n((E, K, H)) / np.sqrt(K) / s[None]]
    w3 = [pack_weight(m, "e2m1") for m in n((E, K, H)) / np.sqrt(K) / s[None] * u[None, None, :]]
    w2 = [pack_weight(m, "e2m1") for m in n((E, H, N)) / np.sqrt(H) / u[None, :, None]]
    x = pack_weight(n((K, T)) * s, "e4m3")
    return {
        "x_words": x[0],
        "x_scales": x[1],
        "w1_words": np.stack([m[0] for m in w1]),
        "w1_scales": np.stack([m[1] for m in w1]),
        "w3_words": np.stack([m[0] for m in w3]),
        "w3_scales": np.stack([m[1] for m in w3]),
        "w2_words": np.stack([m[0] for m in w2]),
        "w2_scales": np.stack([m[1] for m in w2]),
        "gate": np.tile(np.random.uniform(0.2, 1.0, E * C), (N, 1)).astype(np.float32),
        "offs": striped(np.random.permutation(T)[:E * C]),
        "dst": striped(np.random.permutation(T)[:E * C]),
    }


def reference(x_words, x_scales, w1_words, w1_scales, w3_words, w3_scales, w2_words, w2_scales, gate, offs, dst):
    idx = unstriped(offs)
    w1 = np.stack([unpack_weight(w1_words[e], w1_scales[e], "e2m1") for e in range(E)])
    w3 = np.stack([unpack_weight(w3_words[e], w3_scales[e], "e2m1") for e in range(E)])
    w2 = np.stack([unpack_weight(w2_words[e], w2_scales[e], "e2m1") for e in range(E)])
    xq = unpack_weight(x_words, x_scales, "e4m3")[:, idx]
    h = relu(by_expert(w1, xq))
    h = h * by_expert(w3, xq)
    y = by_expert(w2, mxq(h, 0, "e4m3"))
    out = np.zeros((N, T))
    out[:, unstriped(dst)] = f64(gate) * y
    return out

@@ -1,0 +1,214 @@
+from contextlib import ExitStack
+
+import concourse.mybir as mybir
+from concourse.masks import make_identity
+
+K, T, E, C, H, N = 1024, 1024, 8, 128, 512, 256
+FLOPS = 2 * E * C * (2 * K * H + H * N)
+
+F32 = mybir.dt.float32
+BF16 = mybir.dt.bfloat16
+I32 = mybir.dt.int32
+U32 = mybir.dt.uint32
+U16 = mybir.dt.uint16
+U8 = mybir.dt.uint8
+FP8X4 = mybir.dt.float8_e4m3fn_x4
+FP4X4 = mybir.dt.float4_e2m1fn_x4
+MULT = mybir.AluOpType.mult
+RELU = mybir.ActivationFunctionType.Relu
+
+P = 128
+PASSES = K // 512
+PAIR = 2
+SLOTS = PAIR * C
+PAIRS = E // PAIR
+HALVES = N // P
+EARLY = 2
+AHEAD = 3
+
+
+def load_scale_rows(queue, plane, rows):
+    by_r = rows.rearrange("g (q r) n -> r q g n", r=4)
+    for r in range(4):
+        queue.dma_start(out=plane[r:P:32, :, :].bitcast(I32), in_=by_r[r].bitcast(I32))
+
+
+def tile_moe_two_glu_relu_kernel(
+    tc, x_words, x_scales, w1_words, w1_scales, w3_words, w3_scales, w2_words, w2_scales, gate, offs, dst, out
+):
+    nc = tc.nc
+    with ExitStack() as ctx:
+        keep = ctx.enter_context(tc.tile_pool(name="keep", bufs=1))
+        work = ctx.enter_context(tc.tile_pool(name="work", bufs=2))
+        psum = ctx.enter_context(tc.psum_pool(name="psum", bufs=2))
+
+        def zeroed_plane(name, groups, width):
+            plane = keep.tile([P, groups, width], U8, name=name, align_bytes=64)
+            nc.vector.memset(plane[:].rearrange("p g n -> p (g n)").bitcast(I32), 0)
+            return plane
+
+        def load_words(name, words, bufs):
+            groups, width = words.shape[0], words.shape[2]
+            tile = keep.tile([P, groups, width], U8, name=name, align_bytes=64, bufs=bufs)
+            nc.sync.dma_start(out=tile[:].bitcast(I32), in_=words.rearrange("g p b -> p g b").bitcast(I32))
+            return tile
+
+        offs_sb = keep.tile([P, T // 16], U16, name="offs_sb")
+        nc.sync.dma_start(offs_sb[:], offs)
+        x_plane = zeroed_plane("x_plane", PASSES, T)
+        load_scale_rows(nc.scalar, x_plane, x_scales)
+        x_sb = []
+        for s in range(PASSES):
+            tile = keep.tile([P, T], I32, name="x_sb%d" % s, align_bytes=64)
+            nc.sync.dma_start(out=tile[:], in_=x_words[s].rearrange("p t r -> p (t r)").bitcast(I32))
+            x_sb.append(tile)
+
+        def first_layer_planes(queue, name, lo, hi):
+            planes = []
+            for which, scales in (("w1", w1_scales), ("w3", w3_scales)):
+                plane = zeroed_plane(which + name, (hi - lo) * PASSES, H)
+                load_scale_rows(queue, plane, scales[lo:hi].rearrange("e s q n -> (e s) q n"))
+                planes.append(plane)
+            return planes
+
+        early_planes = first_layer_planes(nc.scalar, "_early", 0, EARLY)
+        late_planes = first_layer_planes(nc.sync, "_late", EARLY, E)
+        w2_plane = zeroed_plane("w2_plane", E, N)
+        load_scale_rows(nc.sync, w2_plane, w2_scales.rearrange("e s q n -> (e s) q n"))
+        w13, w2_sb, gates = {}, {}, {}
+
+        def load_first_layer(e):
+            w13[e] = [load_words("w1_sb", w1_words[e], AHEAD), load_words("w3_sb", w3_words[e], AHEAD)]
+
+        def load_second_layer(c):
+            words = w2_words[c * PAIR : (c + 1) * PAIR].rearrange("e s p b -> (e s) p b")
+            w2_sb[c] = load_words("w2_sb", words, 1)
+
+        def load_gate(c):
+            tile = keep.tile([P, SLOTS], F32, name="gate_sb", tag="slots%d" % c, align_bytes=64)
+            nc.sync.dma_start(out=tile[:], in_=gate[0:P, c * SLOTS : (c + 1) * SLOTS])
+            gates[c] = tile
+
+        for e in range(AHEAD):
+            load_first_layer(e)
+        load_second_layer(0)
+        dst_sb = keep.tile([P, T // 16], U16, name="dst_sb")
+        nc.sync.dma_start(dst_sb[:], dst)
+
+        identity = keep.tile([P, P], F32, name="identity")
+        make_identity(nc, identity[:])
+        windows = [keep.tile([P, T], F32, name="window%d" % half) for half in range(HALVES)]
+
+        gathered, hidden, quantised, results = {}, {}, {}, {}
+
+        def gather(c):
+            entries = offs_sb[:, c * SLOTS // 16 : (c + 1) * SLOTS // 16]
+            words, planes = [], []
+            for s in range(PASSES):
+                plane = keep.tile([P, SLOTS], U8, name="xs_%d" % s, align_bytes=64, bufs=3)
+                nc.vector.tensor_copy(plane[:], x_plane[:, s, :].indirect(entries))
+                planes.append(plane)
+            for s in range(PASSES):
+                if s == 0:
+                    tile = keep.tile([P, SLOTS], U32, name="xw_0", tag="slots%d" % c, align_bytes=64)
+                else:
+                    tile = keep.tile([P, SLOTS], U32, name="xw_1", align_bytes=64, bufs=3)
+                nc.vector.tensor_copy(tile[:], x_sb[s][:].bitcast(U32).indirect(entries))
+                words.append(tile)
+            gathered[c] = (words, planes)
+
+        def first_layer(e):
+            words, planes = gathered[e // PAIR]
+            slots = slice((e % PAIR) * C, (e % PAIR + 1) * C)
+            w_planes, first = (early_planes, 0) if e < EARLY else (late_planes, EARLY)
+            banks = []
+            for m, tag in enumerate(("a", "b")):
+                bank = psum.tile([P, H], F32, name=tag)
+                for s in range(PASSES):
+                    nc.tensor.matmul_mx(
+                        out=bank[:],
+                        lhsT=words[s][:, slots].bitcast(FP8X4),
+                        lhsT_scale=planes[s][:, slots],
+                        rhs=w13[e][m][:, s, :].bitcast(FP4X4),
+                        rhs_scale=w_planes[m][:, (e - first) * PASSES + s, :],
+                        start=(s == 0),
+                        stop=(s == PASSES - 1),
+                    )
+                banks.append(bank)
+            if e + AHEAD < E:
+                load_first_layer(e + AHEAD)
+            if e % PAIR == PAIR - 1:
+                load_gate(e // PAIR)
+            a_bank, b_bank = banks
+            relu_a = work.tile([P, 2, P, 2], F32, name="relu_a")
+            nc.scalar.activation(relu_a[:], a_bank[:].rearrange("c (p u j) -> c u p j", u=2, j=2), RELU)
+            h = work.tile([P, 2, P, 2], BF16, name="h", bufs=4)
+            nc.vector.tensor_tensor(h[:], b_bank[:].rearrange("c (p u j) -> c u p j", u=2, j=2), relu_a[:], MULT)
+            hidden[e] = h
+
+        def quantise(c):
+            turned = psum.tile([P, PAIR, 2, C], F32, name="turned")
+            for i in range(PAIR):
+                pairs = hidden[c * PAIR + i][:].rearrange("c u p j -> c u (p j)").bitcast(F32)
+                for u in range(2):
+                    nc.tensor.transpose(turned[:, i, u, :], pairs[:, u, :], identity[:])
+            grouped = work.tile([P, SLOTS * 4], BF16, name="grouped", align_bytes=64)
+            nc.scalar.copy(
+                grouped[:].bitcast(F32).rearrange("p (i c u) -> p i c u", i=PAIR, u=2),
+                turned[:].rearrange("p i u c -> p i c u"),
+            )
+            codes = work.tile([P, SLOTS], U32, name="codes", align_bytes=64)
+            plane = work.tile([P, SLOTS], U8, name="h_plane", align_bytes=64)
+            nc.vector.quantize_mx(out=codes[:].bitcast(FP8X4), scales=plane[:], in_=grouped[:])
+            quantised[c] = (codes, plane)
+
+        def second_layer(c):
+            codes, plane = quantised[c]
+            y_bank = psum.tile([P, HALVES, SLOTS], F32, name="y_bank")
+            for half in range(HALVES):
+                for i in range(PAIR):
+                    e = c * PAIR + i
+                    slots = slice(i * C, (i + 1) * C)
+                    nc.tensor.matmul_mx(
+                        out=y_bank[:, half, slots],
+                        lhsT=w2_sb[c][:, i, half * 2 * P : (half + 1) * 2 * P].bitcast(FP4X4),
+                        lhsT_scale=w2_plane[:, e, half * P : (half + 1) * P],
+                        rhs=codes[:, slots].bitcast(FP8X4),
+                        rhs_scale=plane[:, slots],
+                        start=True,
+                        stop=True,
+                    )
+            if c + 1 < PAIRS:
+                load_second_layer(c + 1)
+            y = work.tile([P, HALVES, SLOTS], F32, name="y")
+            nc.scalar.copy(y[:], y_bank[:])
+            results[c] = y
+
+        def scatter(c, half):
+            entries = dst_sb[:, c * SLOTS // 16 : (c + 1) * SLOTS // 16]
+            nc.vector.tensor_tensor(
+                windows[half][:].indirect(entries),
+                results[c][:, half, :],
+                gates[c][:],
+                MULT,
+            )
+
+        for c in range(PAIRS - 1):
+            gather(c)
+        first_layer(0)
+        first_layer(1)
+        gather(PAIRS - 1)
+        quantise(0)
+        first_layer(2)
+        first_layer(3)
+        for c in range(PAIRS):
+            second_layer(c)
+            scatter(c, 0)
+            if c + 1 < PAIRS:
+                quantise(c + 1)
+            if c + 2 < PAIRS:
+                first_layer((c + 2) * PAIR)
+                first_layer((c + 2) * PAIR + 1)
+            scatter(c, 1)
+        for half in range(HALVES):
+            nc.sync.dma_start(out=out[half * P : (half + 1) * P, :], in_=windows[half][:])

@@ -19,12 +19,10 @@ RELU = mybir.ActivationFunctionType.Relu
 
 P = 128
 PASSES = K // 512
-PAIR = 2
-SLOTS = PAIR * C
-PAIRS = E // PAIR
 HALVES = N // P
-EARLY = 2
-AHEAD = 3
+EARLY = 4
+PAIR_BYTES = 2 * PASSES * 2 * H
+GROUPS = [range(0, 1), range(1, 2), range(2, 4), range(4, 6), range(6, 8)]
 
 
 def load_scale_rows(queue, plane, rows):
@@ -39,176 +37,189 @@ def tile_moe_two_glu_relu_kernel(
     nc = tc.nc
     with ExitStack() as ctx:
         keep = ctx.enter_context(tc.tile_pool(name="keep", bufs=1))
+        shared = ctx.enter_context(tc.tile_pool(name="shared", bufs=1))
         work = ctx.enter_context(tc.tile_pool(name="work", bufs=2))
         psum = ctx.enter_context(tc.psum_pool(name="psum", bufs=2))
 
-        def zeroed_plane(name, groups, width):
-            plane = keep.tile([P, groups, width], U8, name=name, align_bytes=64)
-            nc.vector.memset(plane[:].rearrange("p g n -> p (g n)").bitcast(I32), 0)
+        def zeroed(engine, name, shape):
+            plane = keep.tile(shape, U8, name=name, align_bytes=64)
+            engine.memset(plane[:].bitcast(I32), 0)
             return plane
 
-        def load_words(name, words, bufs):
-            groups, width = words.shape[0], words.shape[2]
-            tile = keep.tile([P, groups, width], U8, name=name, align_bytes=64, bufs=bufs)
-            nc.sync.dma_start(out=tile[:].bitcast(I32), in_=words.rearrange("g p b -> p g b").bitcast(I32))
-            return tile
+        def weight_plane(engine, queue, name, scales, experts):
+            rows = scales[experts.start : experts.stop].rearrange("e s q n -> (e s) q n")
+            plane = zeroed(engine, name, [P, rows.shape[0], rows.shape[2]])
+            load_scale_rows(queue, plane, rows)
+            return plane
 
+        def load_words(queue, tile, words, experts):
+            rows = words[experts.start : experts.stop].rearrange("e s p b -> p (e s) b")
+            queue.dma_start(out=tile.bitcast(I32), in_=rows.bitcast(I32))
+
+        w13 = []
+
+        def pair_tile(tag):
+            return keep.tile([P, 2 * PAIR_BYTES], U8, name="w13_sb", align_bytes=64, tag=tag)
+
+        def load_first_layer(queue, tile, pair):
+            halves = [
+                tile[:, m * PAIR_BYTES : (m + 1) * PAIR_BYTES].rearrange("p (g b) -> p g b", b=2 * H) for m in range(2)
+            ]
+            for half, words in zip(halves, (w1_words, w3_words)):
+                load_words(queue, half, words, range(2 * pair, 2 * pair + 2))
+            w13.append(halves)
+
+        early, late = range(0, EARLY), range(EARLY, E)
         offs_sb = keep.tile([P, T // 16], U16, name="offs_sb")
         nc.sync.dma_start(offs_sb[:], offs)
-        x_plane = zeroed_plane("x_plane", PASSES, T)
-        load_scale_rows(nc.scalar, x_plane, x_scales)
-        x_sb = []
-        for s in range(PASSES):
-            tile = keep.tile([P, T], I32, name="x_sb%d" % s, align_bytes=64)
-            nc.sync.dma_start(out=tile[:], in_=x_words[s].rearrange("p t r -> p (t r)").bitcast(I32))
-            x_sb.append(tile)
-
-        def first_layer_planes(queue, name, lo, hi):
-            planes = []
-            for which, scales in (("w1", w1_scales), ("w3", w3_scales)):
-                plane = zeroed_plane(which + name, (hi - lo) * PASSES, H)
-                load_scale_rows(queue, plane, scales[lo:hi].rearrange("e s q n -> (e s) q n"))
-                planes.append(plane)
-            return planes
-
-        early_planes = first_layer_planes(nc.scalar, "_early", 0, EARLY)
-        late_planes = first_layer_planes(nc.sync, "_late", EARLY, E)
-        w2_plane = zeroed_plane("w2_plane", E, N)
-        load_scale_rows(nc.sync, w2_plane, w2_scales.rearrange("e s q n -> (e s) q n"))
-        w13, w2_sb, gates = {}, {}, {}
-
-        def load_first_layer(e):
-            w13[e] = [load_words("w1_sb", w1_words[e], AHEAD), load_words("w3_sb", w3_words[e], AHEAD)]
-
-        def load_second_layer(c):
-            words = w2_words[c * PAIR : (c + 1) * PAIR].rearrange("e s p b -> (e s) p b")
-            w2_sb[c] = load_words("w2_sb", words, 1)
-
-        def load_gate(c):
-            tile = keep.tile([P, SLOTS], F32, name="gate_sb", tag="slots%d" % c, align_bytes=64)
-            nc.sync.dma_start(out=tile[:], in_=gate[0:P, c * SLOTS : (c + 1) * SLOTS])
-            gates[c] = tile
-
-        for e in range(AHEAD):
-            load_first_layer(e)
-        load_second_layer(0)
+        x_sb = keep.tile([P, PASSES * T], I32, name="x_sb", tag="x_sb", align_bytes=64)
+        nc.gpsimd.dma_start(
+            out=x_sb[:].rearrange("p (s t) -> p s t", s=PASSES),
+            in_=x_words.rearrange("s p t r -> p s (t r)").bitcast(I32),
+        )
+        x_plane = shared.tile([P, T], U8, name="x_plane", align_bytes=64, offset=3 * PAIR_BYTES - T // 2)
+        nc.vector.memset(x_plane[:].bitcast(I32), 0)
+        for q in range(4):
+            nc.sync.dma_start(
+                out=x_plane[32 * q : 32 * q + 4 * PASSES, :].bitcast(I32),
+                in_=x_scales[:, 4 * q : 4 * q + 4, :].bitcast(I32),
+            )
+        early_planes = [
+            weight_plane(nc.vector, nc.sync, "w1_early", w1_scales, early),
+            weight_plane(nc.vector, nc.sync, "w3_early", w3_scales, early),
+        ]
+        moved = zeroed(nc.vector, "moved", [P, T])
         dst_sb = keep.tile([P, T // 16], U16, name="dst_sb")
         nc.sync.dma_start(dst_sb[:], dst)
 
+        load_first_layer(nc.gpsimd, pair_tile("w13"), 0)
         identity = keep.tile([P, P], F32, name="identity")
         make_identity(nc, identity[:])
+        w2_plane = weight_plane(nc.gpsimd, nc.sync, "w2_plane", w2_scales, range(E))
+        late_planes = [
+            weight_plane(nc.gpsimd, nc.sync, "w1_late", w1_scales, late),
+            weight_plane(nc.gpsimd, nc.sync, "w3_late", w3_scales, late),
+        ]
+
         windows = [keep.tile([P, T], F32, name="window%d" % half) for half in range(HALVES)]
 
-        gathered, hidden, quantised, results = {}, {}, {}, {}
+        def entries(lists, experts):
+            return lists[:, experts.start * C // 16 : experts.stop * C // 16]
 
-        def gather(c):
-            entries = offs_sb[:, c * SLOTS // 16 : (c + 1) * SLOTS // 16]
-            words, planes = [], []
+        def part_of(e):
+            return (0, e) if e < EARLY else (1, e - EARLY)
+
+        both = keep.tile([P, T], U8, name="both", align_bytes=64)
+        for part in (range(0, E // 2), range(E // 2, E)):
+            nc.vector.tensor_copy(both[:, part.start * C : part.stop * C], x_plane[:].indirect(entries(offs_sb, part)))
+        for r in range(4):
+            nc.sync.dma_start(out=moved[r:P:32, :].bitcast(I32), in_=both[4 + r : P : 32, :].bitcast(I32))
+        slot_planes = (both, moved)
+        second_wave = shared.tile([P, 3 * PAIR_BYTES], U8, name="second_wave", align_bytes=64, offset=0)
+        w2_sb = second_wave[:, 2 * PAIR_BYTES :].rearrange("p (e b) -> p e b", e=E)
+        load_words(nc.sync, w2_sb, w2_words, range(E))
+        load_first_layer(nc.sync, second_wave, 1)
+        gate_sb = shared.tile([P, T], F32, name="gate_sb", align_bytes=64, offset=3 * PAIR_BYTES)
+        nc.sync.dma_start(out=gate_sb[:], in_=gate[0:P, :])
+
+        slot_words = {}
+        for g, experts in enumerate(GROUPS):
+            tile = keep.tile([P, PASSES, len(experts) * C], U32, name="words", tag="words%d" % g, align_bytes=64)
             for s in range(PASSES):
-                plane = keep.tile([P, SLOTS], U8, name="xs_%d" % s, align_bytes=64, bufs=3)
-                nc.vector.tensor_copy(plane[:], x_plane[:, s, :].indirect(entries))
-                planes.append(plane)
-            for s in range(PASSES):
-                if s == 0:
-                    tile = keep.tile([P, SLOTS], U32, name="xw_0", tag="slots%d" % c, align_bytes=64)
-                else:
-                    tile = keep.tile([P, SLOTS], U32, name="xw_1", align_bytes=64, bufs=3)
-                nc.vector.tensor_copy(tile[:], x_sb[s][:].bitcast(U32).indirect(entries))
-                words.append(tile)
-            gathered[c] = (words, planes)
+                window = x_sb[:, s * T : (s + 1) * T].bitcast(U32)
+                nc.vector.tensor_copy(tile[:, s, :], window.indirect(entries(offs_sb, experts)))
+            for i, e in enumerate(experts):
+                slot_words[e] = [tile[:, s, i * C : (i + 1) * C] for s in range(PASSES)]
+
+        load_first_layer(nc.sync, pair_tile("x_sb"), 2)
+
+        hidden, quantised, results = {}, {}, {}
 
         def first_layer(e):
-            words, planes = gathered[e // PAIR]
-            slots = slice((e % PAIR) * C, (e % PAIR + 1) * C)
-            w_planes, first = (early_planes, 0) if e < EARLY else (late_planes, EARLY)
+            part, i = part_of(e)
+            w_planes = (early_planes, late_planes)[part]
             banks = []
-            for m, tag in enumerate(("a", "b")):
-                bank = psum.tile([P, H], F32, name=tag)
+            for m, (tag, bufs) in enumerate((("a", 2), ("b", 3))):
+                bank = psum.tile([P, H], F32, name=tag, bufs=bufs)
                 for s in range(PASSES):
                     nc.tensor.matmul_mx(
                         out=bank[:],
-                        lhsT=words[s][:, slots].bitcast(FP8X4),
-                        lhsT_scale=planes[s][:, slots],
-                        rhs=w13[e][m][:, s, :].bitcast(FP4X4),
-                        rhs_scale=w_planes[m][:, (e - first) * PASSES + s, :],
+                        lhsT=slot_words[e][s].bitcast(FP8X4),
+                        lhsT_scale=slot_planes[s][:, e * C : (e + 1) * C],
+                        rhs=w13[e // 2][m][:, (e % 2) * PASSES + s, :].bitcast(FP4X4),
+                        rhs_scale=w_planes[m][:, i * PASSES + s, :],
                         start=(s == 0),
                         stop=(s == PASSES - 1),
                     )
                 banks.append(bank)
-            if e + AHEAD < E:
-                load_first_layer(e + AHEAD)
-            if e % PAIR == PAIR - 1:
-                load_gate(e // PAIR)
+            if e == 1:
+                load_first_layer(nc.sync, pair_tile("w13"), 3)
             a_bank, b_bank = banks
-            relu_a = work.tile([P, 2, P, 2], F32, name="relu_a")
-            nc.scalar.activation(relu_a[:], a_bank[:].rearrange("c (p u j) -> c u p j", u=2, j=2), RELU)
-            h = work.tile([P, 2, P, 2], BF16, name="h", bufs=4)
-            nc.vector.tensor_tensor(h[:], b_bank[:].rearrange("c (p u j) -> c u p j", u=2, j=2), relu_a[:], MULT)
+            relu_a = work.tile([P, H], F32, name="relu_a")
+            nc.scalar.activation(relu_a[:], a_bank[:], RELU)
+            h = keep.tile([P, H], BF16, name="h", tag="h%d" % e, align_bytes=64)
+            nc.vector.tensor_tensor(h[:], b_bank[:], relu_a[:], MULT)
             hidden[e] = h
 
-        def quantise(c):
-            turned = psum.tile([P, PAIR, 2, C], F32, name="turned")
-            for i in range(PAIR):
-                pairs = hidden[c * PAIR + i][:].rearrange("c u p j -> c u (p j)").bitcast(F32)
+        def quantise(g):
+            count = len(GROUPS[g])
+            turned = psum.tile([P, count, 2, C], F32, name="turned", bufs=1)
+            for i, e in enumerate(GROUPS[g]):
+                pairs = hidden[e][:].bitcast(F32)
                 for u in range(2):
-                    nc.tensor.transpose(turned[:, i, u, :], pairs[:, u, :], identity[:])
-            grouped = work.tile([P, SLOTS * 4], BF16, name="grouped", align_bytes=64)
+                    nc.tensor.transpose(turned[:, i, u, :], pairs[:, u : H // 2 : 2], identity[:])
+            grouped = work.tile([P, count * C * 4], BF16, name="grouped", align_bytes=64)
             nc.scalar.copy(
-                grouped[:].bitcast(F32).rearrange("p (i c u) -> p i c u", i=PAIR, u=2),
+                grouped[:].bitcast(F32).rearrange("p (i c u) -> p i c u", i=count, u=2),
                 turned[:].rearrange("p i u c -> p i c u"),
             )
-            codes = work.tile([P, SLOTS], U32, name="codes", align_bytes=64)
-            plane = work.tile([P, SLOTS], U8, name="h_plane", align_bytes=64)
+            codes = work.tile([P, count * C], U32, name="codes", align_bytes=64)
+            plane = work.tile([P, count * C], U8, name="h_plane", align_bytes=64)
             nc.vector.quantize_mx(out=codes[:].bitcast(FP8X4), scales=plane[:], in_=grouped[:])
-            quantised[c] = (codes, plane)
+            quantised[g] = (codes, plane)
 
-        def second_layer(c):
-            codes, plane = quantised[c]
-            y_bank = psum.tile([P, HALVES, SLOTS], F32, name="y_bank")
+        def second_layer(g):
+            codes, plane = quantised[g]
+            y_bank = psum.tile([P, HALVES, len(GROUPS[g]) * C], F32, name="y_bank")
             for half in range(HALVES):
-                for i in range(PAIR):
-                    e = c * PAIR + i
-                    slots = slice(i * C, (i + 1) * C)
+                for j, e in enumerate(GROUPS[g]):
+                    slots = slice(j * C, (j + 1) * C)
                     nc.tensor.matmul_mx(
                         out=y_bank[:, half, slots],
-                        lhsT=w2_sb[c][:, i, half * 2 * P : (half + 1) * 2 * P].bitcast(FP4X4),
+                        lhsT=w2_sb[:, e, half * 2 * P : (half + 1) * 2 * P].bitcast(FP4X4),
                         lhsT_scale=w2_plane[:, e, half * P : (half + 1) * P],
                         rhs=codes[:, slots].bitcast(FP8X4),
                         rhs_scale=plane[:, slots],
                         start=True,
                         stop=True,
                     )
-            if c + 1 < PAIRS:
-                load_second_layer(c + 1)
-            y = work.tile([P, HALVES, SLOTS], F32, name="y")
-            nc.scalar.copy(y[:], y_bank[:])
-            results[c] = y
+            results[g] = y_bank
 
-        def scatter(c, half):
-            entries = dst_sb[:, c * SLOTS // 16 : (c + 1) * SLOTS // 16]
+        def scatter(g, half):
+            follower = (g + 1) % len(GROUPS)
+            tag = ("words%d" % follower, "h%d" % GROUPS[follower][-1])[half]
+            y = keep.tile([P, len(GROUPS[g]) * C], F32, name="y", tag=tag, align_bytes=64)
+            nc.scalar.copy(y[:], results[g][:, half, :])
             nc.vector.tensor_tensor(
-                windows[half][:].indirect(entries),
-                results[c][:, half, :],
-                gates[c][:],
+                windows[half][:].indirect(entries(dst_sb, GROUPS[g])),
+                y[:],
+                gate_sb[:, GROUPS[g].start * C : GROUPS[g].stop * C],
                 MULT,
             )
 
-        for c in range(PAIRS - 1):
-            gather(c)
-        first_layer(0)
-        first_layer(1)
-        gather(PAIRS - 1)
+        def first_layers(g):
+            for e in GROUPS[g]:
+                first_layer(e)
+
+        first_layers(0)
         quantise(0)
-        first_layer(2)
-        first_layer(3)
-        for c in range(PAIRS):
-            second_layer(c)
-            scatter(c, 0)
-            if c + 1 < PAIRS:
-                quantise(c + 1)
-            if c + 2 < PAIRS:
-                first_layer((c + 2) * PAIR)
-                first_layer((c + 2) * PAIR + 1)
-            scatter(c, 1)
+        for g in range(len(GROUPS)):
+            second_layer(g)
+            if g + 1 < len(GROUPS):
+                first_layers(g + 1)
+            scatter(g, 0)
+            if g + 1 < len(GROUPS):
+                quantise(g + 1)
+            scatter(g, 1)
         for half in range(HALVES):
             nc.sync.dma_start(out=out[half * P : (half + 1) * P, :], in_=windows[half][:])

@@ -20,9 +20,15 @@ RELU = mybir.ActivationFunctionType.Relu
 P = 128
 PASSES = K // 512
 HALVES = N // P
-EARLY = 4
-PAIR_BYTES = 2 * PASSES * 2 * H
-GROUPS = [range(0, 1), range(1, 2), range(2, 4), range(4, 6), range(6, 8)]
+FIRST_BYTES = PASSES * 2 * H
+SECOND_BYTES = 2 * N
+EXPERT_BYTES = 2 * FIRST_BYTES + SECOND_BYTES
+GATE_ROW = E * C // P
+BATCHES = [range(0, 4), range(4, 8)]
+X_AT = E * EXPERT_BYTES
+X_PLANE_AT = X_AT + PASSES * T * 4
+SLOTS_AT = X_PLANE_AT + T
+SLOT_BYTES = PASSES * C * 4
 
 
 def load_scale_rows(queue, plane, rows):
@@ -41,185 +47,212 @@ def tile_moe_two_glu_relu_kernel(
         work = ctx.enter_context(tc.tile_pool(name="work", bufs=2))
         psum = ctx.enter_context(tc.psum_pool(name="psum", bufs=2))
 
-        def zeroed(engine, name, shape):
+        def zeroed(name, shape):
             plane = keep.tile(shape, U8, name=name, align_bytes=64)
-            engine.memset(plane[:].bitcast(I32), 0)
+            nc.vector.memset(plane[:].bitcast(I32), 0)
             return plane
 
-        def weight_plane(engine, queue, name, scales, experts):
-            rows = scales[experts.start : experts.stop].rearrange("e s q n -> (e s) q n")
-            plane = zeroed(engine, name, [P, rows.shape[0], rows.shape[2]])
-            load_scale_rows(queue, plane, rows)
-            return plane
-
-        def load_words(queue, tile, words, experts):
-            rows = words[experts.start : experts.stop].rearrange("e s p b -> p (e s) b")
-            queue.dma_start(out=tile.bitcast(I32), in_=rows.bitcast(I32))
-
-        w13 = []
-
-        def pair_tile(tag):
-            return keep.tile([P, 2 * PAIR_BYTES], U8, name="w13_sb", align_bytes=64, tag=tag)
-
-        def load_first_layer(queue, tile, pair):
-            halves = [
-                tile[:, m * PAIR_BYTES : (m + 1) * PAIR_BYTES].rearrange("p (g b) -> p g b", b=2 * H) for m in range(2)
-            ]
-            for half, words in zip(halves, (w1_words, w3_words)):
-                load_words(queue, half, words, range(2 * pair, 2 * pair + 2))
-            w13.append(halves)
-
-        early, late = range(0, EARLY), range(EARLY, E)
-        offs_sb = keep.tile([P, T // 16], U16, name="offs_sb")
-        nc.sync.dma_start(offs_sb[:], offs)
-        x_sb = keep.tile([P, PASSES * T], I32, name="x_sb", tag="x_sb", align_bytes=64)
-        nc.gpsimd.dma_start(
-            out=x_sb[:].rearrange("p (s t) -> p s t", s=PASSES),
-            in_=x_words.rearrange("s p t r -> p s (t r)").bitcast(I32),
-        )
-        x_plane = shared.tile([P, T], U8, name="x_plane", align_bytes=64, offset=3 * PAIR_BYTES - T // 2)
-        nc.vector.memset(x_plane[:].bitcast(I32), 0)
-        for q in range(4):
-            nc.sync.dma_start(
-                out=x_plane[32 * q : 32 * q + 4 * PASSES, :].bitcast(I32),
-                in_=x_scales[:, 4 * q : 4 * q + 4, :].bitcast(I32),
-            )
-        early_planes = [
-            weight_plane(nc.vector, nc.sync, "w1_early", w1_scales, early),
-            weight_plane(nc.vector, nc.sync, "w3_early", w3_scales, early),
-        ]
-        moved = zeroed(nc.vector, "moved", [P, T])
-        dst_sb = keep.tile([P, T // 16], U16, name="dst_sb")
-        nc.sync.dma_start(dst_sb[:], dst)
-
-        load_first_layer(nc.gpsimd, pair_tile("w13"), 0)
-        identity = keep.tile([P, P], F32, name="identity")
-        make_identity(nc, identity[:])
-        w2_plane = weight_plane(nc.gpsimd, nc.sync, "w2_plane", w2_scales, range(E))
-        late_planes = [
-            weight_plane(nc.gpsimd, nc.sync, "w1_late", w1_scales, late),
-            weight_plane(nc.gpsimd, nc.sync, "w3_late", w3_scales, late),
-        ]
-
-        windows = [keep.tile([P, T], F32, name="window%d" % half) for half in range(HALVES)]
+        def scale_rows(scales, experts):
+            return scales[experts.start : experts.stop].rearrange("e s q n -> (e s) q n")
 
         def entries(lists, experts):
             return lists[:, experts.start * C // 16 : experts.stop * C // 16]
 
-        def part_of(e):
-            return (0, e) if e < EARLY else (1, e - EARLY)
+        offs_sb = keep.tile([P, T // 16], U16, name="offs_sb")
+        nc.sync.dma_start(offs_sb[:], offs)
+        gate_row = shared.tile([P, GATE_ROW], F32, name="gate_row", align_bytes=64, offset=0)
+        nc.sync.dma_start(out=gate_row[:], in_=gate[0].rearrange("(p j) -> p j", j=GATE_ROW))
+        dst_sb = keep.tile([P, T // 16], U16, name="dst_sb")
+        nc.sync.dma_start(dst_sb[:], dst)
+        x_sb = shared.tile([P, PASSES * T], I32, name="x_sb", align_bytes=64, offset=X_AT)
+        nc.sync.dma_start(
+            out=x_sb[:].rearrange("p (s t) -> p s t", s=PASSES),
+            in_=x_words.rearrange("s p t r -> p s (t r)").bitcast(I32),
+        )
+        x_plane = shared.tile([P, T], U8, name="x_plane", align_bytes=64, offset=X_PLANE_AT)
+        nc.vector.memset(x_plane[:].bitcast(I32), 0)
+        for q in range(4):
+            nc.scalar.dma_start(
+                out=x_plane[32 * q : 32 * q + 4 * PASSES, :].bitcast(I32),
+                in_=x_scales[:, 4 * q : 4 * q + 4, :].bitcast(I32),
+            )
+        first_planes = {}
+        for m in range(2):
+            first_planes[0, m] = zeroed("early%d" % m, [P, len(BATCHES[0]) * PASSES, H])
+        w2_plane = zeroed("w2_plane", [P, E, N])
+
+        identity = keep.tile([P, P], F32, name="identity")
+        make_identity(nc, identity[:])
+
+        gate_sb = keep.tile([P, E * C], F32, name="gate_sb")
+        for u in range(GATE_ROW // 4):
+            spread = psum.tile([P, 4, P], F32, name="spread", tag="y_bank")
+            for j in range(4):
+                column = gate_row[:, 4 * u + j : 4 * u + j + 1].to_broadcast([P, P])
+                nc.tensor.transpose(spread[:, j, :], column, identity[:])
+            nc.scalar.copy(
+                gate_sb[:].rearrange("m (p j) -> m p j", j=GATE_ROW)[:, :, 4 * u : 4 * u + 4],
+                spread[:].rearrange("m j p -> m p j"),
+            )
+
+        weights = shared.tile([P, E * EXPERT_BYTES], U8, name="weights", align_bytes=64, offset=0)
+
+        def first_words(e, m):
+            at = (2 * e + m) * FIRST_BYTES
+            return weights[:, at : at + FIRST_BYTES].rearrange("p (s b) -> p s b", s=PASSES)
+
+        def second_words(experts):
+            at = 2 * E * FIRST_BYTES
+            part = weights[:, at + experts.start * SECOND_BYTES : at + experts.stop * SECOND_BYTES]
+            return part.rearrange("p (e b) -> p e b", b=SECOND_BYTES)
+
+        def load_first_scales(b, m):
+            load_scale_rows(nc.sync, first_planes[b, m], scale_rows((w1_scales, w3_scales)[m], BATCHES[b]))
+
+        def load_first_words(e, m):
+            rows = (w1_words, w3_words)[m][e].rearrange("s p b -> p s b")
+            nc.sync.dma_start(out=first_words(e, m).bitcast(I32), in_=rows.bitcast(I32))
+
+        def load_second_words(experts):
+            rows = w2_words[experts.start : experts.stop].rearrange("e s p b -> p (e s) b")
+            nc.sync.dma_start(out=second_words(experts).bitcast(I32), in_=rows.bitcast(I32))
+
+        for m in range(2):
+            load_first_scales(0, m)
+            load_first_words(0, m)
 
         both = keep.tile([P, T], U8, name="both", align_bytes=64)
         for part in (range(0, E // 2), range(E // 2, E)):
             nc.vector.tensor_copy(both[:, part.start * C : part.stop * C], x_plane[:].indirect(entries(offs_sb, part)))
+        moved = shared.tile([P, T], U8, name="moved", align_bytes=64, offset=X_PLANE_AT)
         for r in range(4):
             nc.sync.dma_start(out=moved[r:P:32, :].bitcast(I32), in_=both[4 + r : P : 32, :].bitcast(I32))
         slot_planes = (both, moved)
-        second_wave = shared.tile([P, 3 * PAIR_BYTES], U8, name="second_wave", align_bytes=64, offset=0)
-        w2_sb = second_wave[:, 2 * PAIR_BYTES :].rearrange("p (e b) -> p e b", e=E)
-        load_words(nc.sync, w2_sb, w2_words, range(E))
-        load_first_layer(nc.sync, second_wave, 1)
-        gate_sb = shared.tile([P, T], F32, name="gate_sb", align_bytes=64, offset=3 * PAIR_BYTES)
-        nc.sync.dma_start(out=gate_sb[:], in_=gate[0:P, :])
 
         slot_words = {}
-        for g, experts in enumerate(GROUPS):
-            tile = keep.tile([P, PASSES, len(experts) * C], U32, name="words", tag="words%d" % g, align_bytes=64)
+        for e in range(E):
+            tile = shared.tile([P, PASSES, C], U32, name="words%d" % e, align_bytes=64, offset=SLOTS_AT + e * SLOT_BYTES)
             for s in range(PASSES):
                 window = x_sb[:, s * T : (s + 1) * T].bitcast(U32)
-                nc.vector.tensor_copy(tile[:, s, :], window.indirect(entries(offs_sb, experts)))
-            for i, e in enumerate(experts):
-                slot_words[e] = [tile[:, s, i * C : (i + 1) * C] for s in range(PASSES)]
+                nc.vector.tensor_copy(tile[:, s, :], window.indirect(entries(offs_sb, range(e, e + 1))))
+            slot_words[e] = [tile[:, s, :] for s in range(PASSES)]
 
-        load_first_layer(nc.sync, pair_tile("x_sb"), 2)
-
-        hidden, quantised, results = {}, {}, {}
-
-        def first_layer(e):
-            part, i = part_of(e)
-            w_planes = (early_planes, late_planes)[part]
-            banks = []
-            for m, (tag, bufs) in enumerate((("a", 2), ("b", 3))):
-                bank = psum.tile([P, H], F32, name=tag, bufs=bufs)
-                for s in range(PASSES):
-                    nc.tensor.matmul_mx(
-                        out=bank[:],
-                        lhsT=slot_words[e][s].bitcast(FP8X4),
-                        lhsT_scale=slot_planes[s][:, e * C : (e + 1) * C],
-                        rhs=w13[e // 2][m][:, (e % 2) * PASSES + s, :].bitcast(FP4X4),
-                        rhs_scale=w_planes[m][:, i * PASSES + s, :],
-                        start=(s == 0),
-                        stop=(s == PASSES - 1),
-                    )
-                banks.append(bank)
-            if e == 1:
-                load_first_layer(nc.sync, pair_tile("w13"), 3)
-            a_bank, b_bank = banks
-            relu_a = work.tile([P, H], F32, name="relu_a")
-            nc.scalar.activation(relu_a[:], a_bank[:], RELU)
-            h = keep.tile([P, H], BF16, name="h", tag="h%d" % e, align_bytes=64)
-            nc.vector.tensor_tensor(h[:], b_bank[:], relu_a[:], MULT)
-            hidden[e] = h
-
-        def quantise(g):
-            count = len(GROUPS[g])
-            turned = psum.tile([P, count, 2, C], F32, name="turned", bufs=1)
-            for i, e in enumerate(GROUPS[g]):
-                pairs = hidden[e][:].bitcast(F32)
-                for u in range(2):
-                    nc.tensor.transpose(turned[:, i, u, :], pairs[:, u : H // 2 : 2], identity[:])
-            grouped = work.tile([P, count * C * 4], BF16, name="grouped", align_bytes=64)
-            nc.scalar.copy(
-                grouped[:].bitcast(F32).rearrange("p (i c u) -> p i c u", i=count, u=2),
-                turned[:].rearrange("p i u c -> p i c u"),
+        for m in range(2):
+            first_planes[1, m] = shared.tile(
+                [P, len(BATCHES[1]) * PASSES, H], U8, name="late%d" % m, align_bytes=64, offset=X_AT + m * T * 4
             )
-            codes = work.tile([P, count * C], U32, name="codes", align_bytes=64)
-            plane = work.tile([P, count * C], U8, name="h_plane", align_bytes=64)
-            nc.vector.quantize_mx(out=codes[:].bitcast(FP8X4), scales=plane[:], in_=grouped[:])
-            quantised[g] = (codes, plane)
 
-        def second_layer(g):
-            codes, plane = quantised[g]
-            y_bank = psum.tile([P, HALVES, len(GROUPS[g]) * C], F32, name="y_bank")
+        load_first_words(1, 0)
+        for e in range(1, E):
+            if e + 1 == BATCHES[1].start:
+                load_first_scales(1, 0)
+            if e + 1 < E:
+                load_first_words(e + 1, 0)
+            if e == BATCHES[1].start:
+                load_first_scales(1, 1)
+            load_first_words(e, 1)
+            if e == 1:
+                load_scale_rows(nc.sync, w2_plane, scale_rows(w2_scales, range(E)))
+                load_second_words(BATCHES[0])
+            if e == BATCHES[1].start:
+                load_second_words(BATCHES[1])
+
+        windows = [keep.tile([P, T], F32, name="window%d" % half) for half in range(HALVES)]
+        banks, rectified, hidden, grouped, quantised, results, staged = {}, {}, {}, {}, {}, {}, {}
+
+        def first_layer(e, m):
+            b = [e in batch for batch in BATCHES].index(True)
+            bank = psum.tile([P, H], F32, name="ab"[m], bufs=2 - m)
+            for s in range(PASSES):
+                nc.tensor.matmul_mx(
+                    out=bank[:],
+                    lhsT=slot_words[e][s].bitcast(FP8X4),
+                    lhsT_scale=slot_planes[s][:, e * C : (e + 1) * C],
+                    rhs=first_words(e, m)[:, s, :].bitcast(FP4X4),
+                    rhs_scale=first_planes[b, m][:, (e - BATCHES[b].start) * PASSES + s, :],
+                    start=(s == 0),
+                    stop=(s == PASSES - 1),
+                )
+            banks[e, m] = bank
+
+        def rectify(e):
+            first_layer(e, 0)
+            rectified[e] = work.tile([P, H], F32, name="relu_a", align_bytes=64)
+            nc.scalar.activation(rectified[e][:], banks[e, 0][:], RELU)
+
+        def product(e):
+            hidden[e] = work.tile([P, H], BF16, name="h", align_bytes=64)
+            nc.vector.tensor_tensor(hidden[e][:], banks[e, 1][:], rectified[e][:], MULT)
+
+        def turn(e):
+            turned = psum.tile([P, 2, C], F32, name="turned", bufs=1)
+            pairs = hidden[e][:].bitcast(F32)
+            for u in range(2):
+                nc.tensor.transpose(turned[:, u, :], pairs[:, u : H // 2 : 2], identity[:])
+            grouped[e] = keep.tile([P, C * 4], BF16, name="grouped", tag="group%d" % (e % 2), align_bytes=64)
+            nc.scalar.copy(
+                grouped[e][:].bitcast(F32).rearrange("p (c u) -> p c u", u=2), turned[:].rearrange("p u c -> p c u")
+            )
+
+        def second_layer(e):
+            if e + 1 < E:
+                at = SLOTS_AT + (e + 1) * SLOT_BYTES
+                codes = shared.tile([P, C], U32, name="codes%d" % e, align_bytes=64, offset=at)
+            else:
+                codes = work.tile([P, C], U32, name="codes", align_bytes=64)
+            plane = work.tile([P, C], U8, name="h_plane", align_bytes=64)
+            nc.vector.quantize_mx(out=codes[:].bitcast(FP8X4), scales=plane[:], in_=grouped[e][:])
+            results[e] = psum.tile([P, HALVES, C], F32, name="y_bank", tag="y_bank")
             for half in range(HALVES):
-                for j, e in enumerate(GROUPS[g]):
-                    slots = slice(j * C, (j + 1) * C)
-                    nc.tensor.matmul_mx(
-                        out=y_bank[:, half, slots],
-                        lhsT=w2_sb[:, e, half * 2 * P : (half + 1) * 2 * P].bitcast(FP4X4),
-                        lhsT_scale=w2_plane[:, e, half * P : (half + 1) * P],
-                        rhs=codes[:, slots].bitcast(FP8X4),
-                        rhs_scale=plane[:, slots],
-                        start=True,
-                        stop=True,
-                    )
-            results[g] = y_bank
+                nc.tensor.matmul_mx(
+                    out=results[e][:, half, :],
+                    lhsT=second_words(range(e, e + 1))[:, 0, half * 2 * P : (half + 1) * 2 * P].bitcast(FP4X4),
+                    lhsT_scale=w2_plane[:, e, half * P : (half + 1) * P],
+                    rhs=codes[:].bitcast(FP8X4),
+                    rhs_scale=plane[:],
+                    start=True,
+                    stop=True,
+                )
 
-        def scatter(g, half):
-            follower = (g + 1) % len(GROUPS)
-            tag = ("words%d" % follower, "h%d" % GROUPS[follower][-1])[half]
-            y = keep.tile([P, len(GROUPS[g]) * C], F32, name="y", tag=tag, align_bytes=64)
-            nc.scalar.copy(y[:], results[g][:, half, :])
+        def stage(e, half):
+            if half == 1 and e + 2 < E:
+                at = SLOTS_AT + (e + 2) * SLOT_BYTES + C * 4
+                y = shared.tile([P, C], F32, name="y%d" % e, align_bytes=64, offset=at)
+            elif half == 1 and e + 2 == E:
+                y = keep.tile([P, C], F32, name="y", tag="group%d" % ((e + 1) % 2), align_bytes=64)
+            else:
+                y = work.tile([P, C], F32, name="y_low", align_bytes=64)
+            nc.scalar.copy(y[:], results[e][:, half, :])
+            staged[e, half] = y
+
+        def scatter(e, half):
             nc.vector.tensor_tensor(
-                windows[half][:].indirect(entries(dst_sb, GROUPS[g])),
-                y[:],
-                gate_sb[:, GROUPS[g].start * C : GROUPS[g].stop * C],
+                windows[half][:].indirect(entries(dst_sb, range(e, e + 1))),
+                staged[e, half][:],
+                gate_sb[:, e * C : (e + 1) * C],
                 MULT,
             )
 
-        def first_layers(g):
-            for e in GROUPS[g]:
-                first_layer(e)
-
-        first_layers(0)
-        quantise(0)
-        for g in range(len(GROUPS)):
-            second_layer(g)
-            if g + 1 < len(GROUPS):
-                first_layers(g + 1)
-            scatter(g, 0)
-            if g + 1 < len(GROUPS):
-                quantise(g + 1)
-            scatter(g, 1)
-        for half in range(HALVES):
-            nc.sync.dma_start(out=out[half * P : (half + 1) * P, :], in_=windows[half][:])
+        rectify(0)
+        first_layer(0, 1)
+        rectify(1)
+        product(0)
+        for e in range(E):
+            turn(e)
+            if e + 1 < E:
+                first_layer(e + 1, 1)
+            if e + 2 < E:
+                rectify(e + 2)
+            second_layer(e)
+            if e > 0:
+                stage(e - 1, 1)
+            stage(e, 0)
+            if e + 1 < E:
+                product(e + 1)
+            if e > 0:
+                scatter(e - 1, 1)
+            scatter(e, 0)
+        nc.sync.dma_start(out=out[0:P, :], in_=windows[0][:])
+        stage(E - 1, 1)
+        scatter(E - 1, 1)
+        nc.sync.dma_start(out=out[P : 2 * P, :], in_=windows[1][:])

@@ -25,10 +25,11 @@ SECOND_BYTES = 2 * N
 EXPERT_BYTES = 2 * FIRST_BYTES + SECOND_BYTES
 GATE_ROW = E * C // P
 BATCHES = [range(0, 4), range(4, 8)]
+LOADS = [range(0, 1), range(1, 3), range(3, 4), range(4, 5), range(5, 6), range(6, 8)]
 X_AT = E * EXPERT_BYTES
-X_PLANE_AT = X_AT + PASSES * T * 4
-SLOTS_AT = X_PLANE_AT + T
-SLOT_BYTES = PASSES * C * 4
+SLOTS_AT = X_AT + PASSES * T * 4
+WORD_BYTES = C * 4
+SLOT_BYTES = 2 * WORD_BYTES
 
 
 def load_scale_rows(queue, plane, rows):
@@ -61,32 +62,29 @@ def tile_moe_two_glu_relu_kernel(
         offs_sb = keep.tile([P, T // 16], U16, name="offs_sb")
         nc.sync.dma_start(offs_sb[:], offs)
         gate_row = shared.tile([P, GATE_ROW], F32, name="gate_row", align_bytes=64, offset=0)
+        identity = keep.tile([P, P], F32, name="identity")
+        make_identity(nc, identity[:])
         nc.sync.dma_start(out=gate_row[:], in_=gate[0].rearrange("(p j) -> p j", j=GATE_ROW))
         dst_sb = keep.tile([P, T // 16], U16, name="dst_sb")
         nc.sync.dma_start(dst_sb[:], dst)
-        x_sb = shared.tile([P, PASSES * T], I32, name="x_sb", align_bytes=64, offset=X_AT)
-        nc.sync.dma_start(
-            out=x_sb[:].rearrange("p (s t) -> p s t", s=PASSES),
-            in_=x_words.rearrange("s p t r -> p s (t r)").bitcast(I32),
-        )
-        x_plane = shared.tile([P, T], U8, name="x_plane", align_bytes=64, offset=X_PLANE_AT)
-        nc.vector.memset(x_plane[:].bitcast(I32), 0)
-        for q in range(4):
-            nc.scalar.dma_start(
-                out=x_plane[32 * q : 32 * q + 4 * PASSES, :].bitcast(I32),
-                in_=x_scales[:, 4 * q : 4 * q + 4, :].bitcast(I32),
-            )
+        x_sb = []
+        for s in range(PASSES):
+            tile = shared.tile([P, T], I32, name="x_sb%d" % s, align_bytes=64, offset=X_AT + s * T * 4)
+            nc.sync.dma_start(out=tile[:], in_=x_words[s].rearrange("p t r -> p (t r)").bitcast(I32))
+            x_sb.append(tile)
+        x_plane = zeroed("x_plane", [P, T])
+        x_rows = x_scales.rearrange("s (q r) t -> r q s t", r=4)
+        for r in range(4):
+            nc.scalar.dma_start(out=x_plane[r:P:16, :].bitcast(I32), in_=x_rows[r].bitcast(I32))
         first_planes = {}
         for m in range(2):
             first_planes[0, m] = zeroed("early%d" % m, [P, len(BATCHES[0]) * PASSES, H])
+        moved = [zeroed("moved%d" % b, [P, len(batch) * C]) for b, batch in enumerate(BATCHES)]
         w2_plane = zeroed("w2_plane", [P, E, N])
-
-        identity = keep.tile([P, P], F32, name="identity")
-        make_identity(nc, identity[:])
 
         gate_sb = keep.tile([P, E * C], F32, name="gate_sb")
         for u in range(GATE_ROW // 4):
-            spread = psum.tile([P, 4, P], F32, name="spread", tag="y_bank")
+            spread = psum.tile([P, 4, P], F32, name="spread", tag="b%d" % u, bufs=1)
             for j in range(4):
                 column = gate_row[:, 4 * u + j : 4 * u + j + 1].to_broadcast([P, P])
                 nc.tensor.transpose(spread[:, j, :], column, identity[:])
@@ -97,9 +95,10 @@ def tile_moe_two_glu_relu_kernel(
 
         weights = shared.tile([P, E * EXPERT_BYTES], U8, name="weights", align_bytes=64, offset=0)
 
-        def first_words(e, m):
-            at = (2 * e + m) * FIRST_BYTES
-            return weights[:, at : at + FIRST_BYTES].rearrange("p (s b) -> p s b", s=PASSES)
+        def first_words(experts, m):
+            at = m * E * FIRST_BYTES
+            part = weights[:, at + experts.start * FIRST_BYTES : at + experts.stop * FIRST_BYTES]
+            return part.rearrange("p (g b) -> p g b", b=2 * H)
 
         def second_words(experts):
             at = 2 * E * FIRST_BYTES
@@ -109,9 +108,9 @@ def tile_moe_two_glu_relu_kernel(
         def load_first_scales(b, m):
             load_scale_rows(nc.sync, first_planes[b, m], scale_rows((w1_scales, w3_scales)[m], BATCHES[b]))
 
-        def load_first_words(e, m):
-            rows = (w1_words, w3_words)[m][e].rearrange("s p b -> p s b")
-            nc.sync.dma_start(out=first_words(e, m).bitcast(I32), in_=rows.bitcast(I32))
+        def load_first_words(experts, m):
+            rows = (w1_words, w3_words)[m][experts.start : experts.stop].rearrange("e s p b -> p (e s) b")
+            nc.sync.dma_start(out=first_words(experts, m).bitcast(I32), in_=rows.bitcast(I32))
 
         def load_second_words(experts):
             rows = w2_words[experts.start : experts.stop].rearrange("e s p b -> p (e s) b")
@@ -119,56 +118,80 @@ def tile_moe_two_glu_relu_kernel(
 
         for m in range(2):
             load_first_scales(0, m)
-            load_first_words(0, m)
+            load_first_words(LOADS[0], m)
 
-        both = keep.tile([P, T], U8, name="both", align_bytes=64)
-        for part in (range(0, E // 2), range(E // 2, E)):
-            nc.vector.tensor_copy(both[:, part.start * C : part.stop * C], x_plane[:].indirect(entries(offs_sb, part)))
-        moved = shared.tile([P, T], U8, name="moved", align_bytes=64, offset=X_PLANE_AT)
-        for r in range(4):
-            nc.sync.dma_start(out=moved[r:P:32, :].bitcast(I32), in_=both[4 + r : P : 32, :].bitcast(I32))
-        slot_planes = (both, moved)
+        both = {}
+
+        def gather_scales(b, tile):
+            nc.vector.tensor_copy(tile[:], x_plane[:].indirect(entries(offs_sb, BATCHES[b])))
+            for r in range(4):
+                nc.sync.dma_start(out=moved[b][r:P:32, :].bitcast(I32), in_=tile[16 + r : P : 32, :].bitcast(I32))
+            both[b] = tile
+
+        gather_scales(0, keep.tile([P, len(BATCHES[0]) * C], U8, name="both0", align_bytes=64))
 
         slot_words = {}
-        for e in range(E):
-            tile = shared.tile([P, PASSES, C], U32, name="words%d" % e, align_bytes=64, offset=SLOTS_AT + e * SLOT_BYTES)
-            for s in range(PASSES):
-                window = x_sb[:, s * T : (s + 1) * T].bitcast(U32)
-                nc.vector.tensor_copy(tile[:, s, :], window.indirect(entries(offs_sb, range(e, e + 1))))
-            slot_words[e] = [tile[:, s, :] for s in range(PASSES)]
 
-        for m in range(2):
+        def over_slots(shape, dtype, name, e, at):
+            return shared.tile(shape, dtype, name=name, align_bytes=64, offset=SLOTS_AT + e * SLOT_BYTES + at)
+
+        def gather_words(s, experts, tile):
+            nc.vector.tensor_copy(tile[:], x_sb[s][:].bitcast(U32).indirect(entries(offs_sb, experts)))
+            for i, e in enumerate(experts):
+                slot_words[e, s] = tile[:, i * C : (i + 1) * C]
+
+        def gather_second_pass(e):
+            gather_words(1, range(e, e + 1), over_slots([P, C], U32, "words%d" % e, e, WORD_BYTES // 2))
+
+        for b, batch in enumerate(BATCHES):
+            gather_words(0, batch, keep.tile([P, len(batch) * C], U32, name="batch%d" % b, align_bytes=64))
+            for e in batch:
+                gather_second_pass(e)
+
+        def load_late_scales(m):
             first_planes[1, m] = shared.tile(
                 [P, len(BATCHES[1]) * PASSES, H], U8, name="late%d" % m, align_bytes=64, offset=X_AT + m * T * 4
             )
+            load_first_scales(1, m)
 
-        load_first_words(1, 0)
-        for e in range(1, E):
-            if e + 1 == BATCHES[1].start:
-                load_first_scales(1, 0)
-            if e + 1 < E:
-                load_first_words(e + 1, 0)
-            if e == BATCHES[1].start:
-                load_first_scales(1, 1)
-            load_first_words(e, 1)
-            if e == 1:
+        def load_step(experts):
+            load_first_words(experts, 0)
+            if experts.stop == BATCHES[1].start:
+                load_late_scales(0)
+            if experts.start == BATCHES[1].start:
+                load_late_scales(1)
+            load_first_words(experts, 1)
+            if 2 in experts:
                 load_scale_rows(nc.sync, w2_plane, scale_rows(w2_scales, range(E)))
                 load_second_words(BATCHES[0])
-            if e == BATCHES[1].start:
+            if experts.start == BATCHES[1].start:
                 load_second_words(BATCHES[1])
+
+        for experts in LOADS[1:3]:
+            load_step(experts)
 
         windows = [keep.tile([P, T], F32, name="window%d" % half) for half in range(HALVES)]
         banks, rectified, hidden, grouped, quantised, results, staged = {}, {}, {}, {}, {}, {}, {}
 
+        def woven(bank):
+            return bank[:].rearrange("c (p u v) -> c u p v", u=2, v=2)
+
+        def split(tile):
+            return tile[:].rearrange("c (u p v) -> c u p v", u=2, v=2)
+
         def first_layer(e, m):
             b = [e in batch for batch in BATCHES].index(True)
-            bank = psum.tile([P, H], F32, name="ab"[m], bufs=2 - m)
+            if m == 0:
+                tag = "spare" if e == 2 else "turn%d" % (e % 2)
+            else:
+                tag = "b1" if e == 1 else "b0"
+            bank = psum.tile([P, H], F32, name="sums", tag=tag, bufs=1)
             for s in range(PASSES):
                 nc.tensor.matmul_mx(
                     out=bank[:],
-                    lhsT=slot_words[e][s].bitcast(FP8X4),
-                    lhsT_scale=slot_planes[s][:, e * C : (e + 1) * C],
-                    rhs=first_words(e, m)[:, s, :].bitcast(FP4X4),
+                    lhsT=slot_words[e, s].bitcast(FP8X4),
+                    lhsT_scale=(both, moved)[s][b][:, (e - BATCHES[b].start) * C : (e - BATCHES[b].start + 1) * C],
+                    rhs=first_words(range(e, e + 1), m)[:, s, :].bitcast(FP4X4),
                     rhs_scale=first_planes[b, m][:, (e - BATCHES[b].start) * PASSES + s, :],
                     start=(s == 0),
                     stop=(s == PASSES - 1),
@@ -177,35 +200,38 @@ def tile_moe_two_glu_relu_kernel(
 
         def rectify(e):
             first_layer(e, 0)
-            rectified[e] = work.tile([P, H], F32, name="relu_a", align_bytes=64)
-            nc.scalar.activation(rectified[e][:], banks[e, 0][:], RELU)
+            if e == 0:
+                rectified[e] = over_slots([P, H], F32, "first_relu", E, 0)
+            else:
+                rectified[e] = work.tile([P, H], F32, name="relu_a", align_bytes=64)
+            nc.scalar.activation(split(rectified[e]), woven(banks[e, 0]), RELU)
 
         def product(e):
-            hidden[e] = work.tile([P, H], BF16, name="h", align_bytes=64)
-            nc.vector.tensor_tensor(hidden[e][:], banks[e, 1][:], rectified[e][:], MULT)
+            hidden[e] = keep.tile([P, H], BF16, name="h", tag="h%d" % (e % 2), align_bytes=64)
+            nc.vector.tensor_tensor(split(hidden[e]), woven(banks[e, 1]), split(rectified[e]), MULT)
 
         def turn(e):
-            turned = psum.tile([P, 2, C], F32, name="turned", bufs=1)
+            turned = psum.tile([P, 2, C], F32, name="turned", tag="turn%d" % (e % 2), bufs=1)
             pairs = hidden[e][:].bitcast(F32)
             for u in range(2):
-                nc.tensor.transpose(turned[:, u, :], pairs[:, u : H // 2 : 2], identity[:])
-            grouped[e] = keep.tile([P, C * 4], BF16, name="grouped", tag="group%d" % (e % 2), align_bytes=64)
+                nc.tensor.transpose(turned[:, u, :], pairs[:, u * P : (u + 1) * P], identity[:])
+            grouped[e] = work.tile([P, C * 4], BF16, name="grouped", align_bytes=64)
             nc.scalar.copy(
                 grouped[e][:].bitcast(F32).rearrange("p (c u) -> p c u", u=2), turned[:].rearrange("p u c -> p c u")
             )
 
-        def second_layer(e):
-            if e + 1 < E:
-                at = SLOTS_AT + (e + 1) * SLOT_BYTES
-                codes = shared.tile([P, C], U32, name="codes%d" % e, align_bytes=64, offset=at)
-            else:
-                codes = work.tile([P, C], U32, name="codes", align_bytes=64)
+        def quantise(e):
+            codes = work.tile([P, C], U32, name="codes", align_bytes=64)
             plane = work.tile([P, C], U8, name="h_plane", align_bytes=64)
             nc.vector.quantize_mx(out=codes[:].bitcast(FP8X4), scales=plane[:], in_=grouped[e][:])
-            results[e] = psum.tile([P, HALVES, C], F32, name="y_bank", tag="y_bank")
+            quantised[e] = (codes, plane)
+
+        def second_layer(e):
+            codes, plane = quantised[e]
+            bank = psum.tile([P, HALVES, C], F32, name="y_bank", bufs=1)
             for half in range(HALVES):
                 nc.tensor.matmul_mx(
-                    out=results[e][:, half, :],
+                    out=bank[:, half, :],
                     lhsT=second_words(range(e, e + 1))[:, 0, half * 2 * P : (half + 1) * 2 * P].bitcast(FP4X4),
                     lhsT_scale=w2_plane[:, e, half * P : (half + 1) * P],
                     rhs=codes[:].bitcast(FP8X4),
@@ -213,46 +239,44 @@ def tile_moe_two_glu_relu_kernel(
                     start=True,
                     stop=True,
                 )
-
-        def stage(e, half):
-            if half == 1 and e + 2 < E:
-                at = SLOTS_AT + (e + 2) * SLOT_BYTES + C * 4
-                y = shared.tile([P, C], F32, name="y%d" % e, align_bytes=64, offset=at)
-            elif half == 1 and e + 2 == E:
-                y = keep.tile([P, C], F32, name="y", tag="group%d" % ((e + 1) % 2), align_bytes=64)
+            if e + 2 < E:
+                staged[e] = over_slots([P, HALVES, C], F32, "y%d" % e, e + 2, 0)
             else:
-                y = work.tile([P, C], F32, name="y_low", align_bytes=64)
-            nc.scalar.copy(y[:], results[e][:, half, :])
-            staged[e, half] = y
+                staged[e] = keep.tile([P, HALVES, C], F32, name="y", tag="h%d" % ((e + 1) % 2), align_bytes=64)
+            nc.scalar.copy(staged[e][:], bank[:])
 
-        def scatter(e, half):
-            nc.vector.tensor_tensor(
-                windows[half][:].indirect(entries(dst_sb, range(e, e + 1))),
-                staged[e, half][:],
-                gate_sb[:, e * C : (e + 1) * C],
-                MULT,
-            )
+        def scatter(e):
+            for half in range(HALVES):
+                nc.vector.tensor_tensor(
+                    windows[half][:].indirect(entries(dst_sb, range(e, e + 1))),
+                    staged[e][:, half, :],
+                    gate_sb[:, e * C : (e + 1) * C],
+                    MULT,
+                )
 
-        rectify(0)
-        first_layer(0, 1)
-        rectify(1)
+        for e in range(2):
+            rectify(e)
+            first_layer(e, 1)
         product(0)
-        for e in range(E):
-            turn(e)
+        gather_scales(1, over_slots([P, len(BATCHES[1]) * C], U8, "both1", E, 0))
+        product(1)
+        for experts in LOADS[3:]:
+            load_step(experts)
+        rectify(2)
+        turn(0)
+        quantise(0)
+        for e in range(1, E + 1):
+            if e < E:
+                turn(e)
             if e + 1 < E:
                 first_layer(e + 1, 1)
+            second_layer(e - 1)
             if e + 2 < E:
                 rectify(e + 2)
-            second_layer(e)
-            if e > 0:
-                stage(e - 1, 1)
-            stage(e, 0)
             if e + 1 < E:
                 product(e + 1)
-            if e > 0:
-                scatter(e - 1, 1)
-            scatter(e, 0)
-        nc.sync.dma_start(out=out[0:P, :], in_=windows[0][:])
-        stage(E - 1, 1)
-        scatter(E - 1, 1)
-        nc.sync.dma_start(out=out[P : 2 * P, :], in_=windows[1][:])
+            if e < E:
+                quantise(e)
+            scatter(e - 1)
+        for half in range(HALVES):
+            nc.sync.dma_start(out=out[half * P : (half + 1) * P, :], in_=windows[half][:])

@@ -16,25 +16,24 @@ FP8X4 = mybir.dt.float8_e4m3fn_x4
 FP4X4 = mybir.dt.float4_e2m1fn_x4
 MULT = mybir.AluOpType.mult
 RELU = mybir.ActivationFunctionType.Relu
+COPY = mybir.ActivationFunctionType.Copy
 
 P = 128
 PASSES = K // 512
 HALVES = N // P
-FIRST_BYTES = PASSES * 2 * H
-SECOND_BYTES = 2 * N
-EXPERT_BYTES = 2 * FIRST_BYTES + SECOND_BYTES
 GATE_ROW = E * C // P
-BATCHES = [range(0, 4), range(4, 8)]
-LOADS = [range(0, 1), range(1, 3), range(3, 4), range(4, 5), range(5, 6), range(6, 8)]
-X_AT = E * EXPERT_BYTES
-SLOTS_AT = X_AT + PASSES * T * 4
-WORD_BYTES = C * 4
-SLOT_BYTES = 2 * WORD_BYTES
+PAIR = 2 * C
+EARLY = range(0, 4)
+LATE = range(4, E)
+RELU_BYTES = H * 4
+WINDOWS_AT = E * RELU_BYTES
+LOADS = [range(0, 1), range(1, 3), range(3, 5), range(5, 8)]
+FREE_GATHERS = 4
 
 
-def load_scale_rows(queue, plane, rows):
+def load_scale_rows(queue, plane, rows, which=range(4)):
     by_r = rows.rearrange("g (q r) n -> r q g n", r=4)
-    for r in range(4):
+    for r in which:
         queue.dma_start(out=plane[r:P:32, :, :].bitcast(I32), in_=by_r[r].bitcast(I32))
 
 
@@ -46,7 +45,7 @@ def tile_moe_two_glu_relu_kernel(
         keep = ctx.enter_context(tc.tile_pool(name="keep", bufs=1))
         shared = ctx.enter_context(tc.tile_pool(name="shared", bufs=1))
         work = ctx.enter_context(tc.tile_pool(name="work", bufs=2))
-        psum = ctx.enter_context(tc.psum_pool(name="psum", bufs=2))
+        psum = ctx.enter_context(tc.psum_pool(name="psum", bufs=1))
 
         def zeroed(name, shape):
             plane = keep.tile(shape, U8, name=name, align_bytes=64)
@@ -56,35 +55,76 @@ def tile_moe_two_glu_relu_kernel(
         def scale_rows(scales, experts):
             return scales[experts.start : experts.stop].rearrange("e s q n -> (e s) q n")
 
-        def entries(lists, experts):
-            return lists[:, experts.start * C // 16 : experts.stop * C // 16]
+        def entries(lists, first, count):
+            return lists[:, first // 16 : (first + count) // 16]
+
+        x_plane = keep.tile([P, PASSES, T], U8, name="x_plane", align_bytes=64)
+        nc.gpsimd.memset(x_plane[:].bitcast(I32), 0)
+        early = [zeroed("early%d" % m, [P, len(EARLY) * PASSES, H]) for m in range(2)]
+        w2_plane = zeroed("w2_plane", [P, E, N])
+        late = [zeroed("late%d" % m, [P, len(LATE) * PASSES, H]) for m in range(2)]
+        identity = keep.tile([P, P], F32, name="identity")
+        make_identity(nc, identity[:])
 
         offs_sb = keep.tile([P, T // 16], U16, name="offs_sb")
         nc.sync.dma_start(offs_sb[:], offs)
-        gate_row = shared.tile([P, GATE_ROW], F32, name="gate_row", align_bytes=64, offset=0)
-        identity = keep.tile([P, P], F32, name="identity")
-        make_identity(nc, identity[:])
-        nc.sync.dma_start(out=gate_row[:], in_=gate[0].rearrange("(p j) -> p j", j=GATE_ROW))
         dst_sb = keep.tile([P, T // 16], U16, name="dst_sb")
         nc.sync.dma_start(dst_sb[:], dst)
-        x_sb = []
-        for s in range(PASSES):
-            tile = shared.tile([P, T], I32, name="x_sb%d" % s, align_bytes=64, offset=X_AT + s * T * 4)
-            nc.sync.dma_start(out=tile[:], in_=x_words[s].rearrange("p t r -> p (t r)").bitcast(I32))
-            x_sb.append(tile)
-        x_plane = zeroed("x_plane", [P, T])
-        x_rows = x_scales.rearrange("s (q r) t -> r q s t", r=4)
-        for r in range(4):
-            nc.scalar.dma_start(out=x_plane[r:P:16, :].bitcast(I32), in_=x_rows[r].bitcast(I32))
-        first_planes = {}
+        load_scale_rows(nc.sync, x_plane, x_scales)
+        load_scale_rows(nc.sync, early[0], scale_rows(w1_scales, EARLY), range(0, 1))
+        x_sb = keep.tile([P, PASSES, T], I32, name="x_sb", align_bytes=64)
+        nc.sync.dma_start(out=x_sb[:], in_=x_words.rearrange("s p t r -> p s (t r)").bitcast(I32))
+        load_scale_rows(nc.sync, early[0], scale_rows(w1_scales, EARLY), range(1, 4))
+        load_scale_rows(nc.sync, early[1], scale_rows(w3_scales, EARLY))
+        gate_row = keep.tile([P, GATE_ROW], F32, name="gate_row")
+        nc.gpsimd.dma_start(out=gate_row[:], in_=gate[0].rearrange("(p j) -> p j", j=GATE_ROW))
+        load_scale_rows(nc.gpsimd, w2_plane, scale_rows(w2_scales, range(E)))
         for m in range(2):
-            first_planes[0, m] = zeroed("early%d" % m, [P, len(BATCHES[0]) * PASSES, H])
-        moved = [zeroed("moved%d" % b, [P, len(batch) * C]) for b, batch in enumerate(BATCHES)]
-        w2_plane = zeroed("w2_plane", [P, E, N])
+            load_scale_rows(nc.gpsimd, late[m], scale_rows((w1_scales, w3_scales)[m], LATE))
+
+        first_words = {}
+
+        def load_first(experts, m):
+            name = "w%d_%d" % (2 * m + 1, experts.start)
+            tile = keep.tile([P, len(experts) * PASSES, 2 * H], U8, name=name, align_bytes=64)
+            rows = (w1_words, w3_words)[m][experts.start : experts.stop].rearrange("e s p b -> p (e s) b")
+            nc.sync.dma_start(out=tile[:].bitcast(I32), in_=rows.bitcast(I32))
+            for i, e in enumerate(experts):
+                first_words[e, m] = tile[:, i * PASSES : (i + 1) * PASSES, :]
+
+        for experts in LOADS:
+            for m in range(2):
+                load_first(experts, m)
+            if 2 in experts:
+                at = WINDOWS_AT + T * 2
+                second_words = shared.tile([P, E, 2 * N], U8, name="w2", align_bytes=64, offset=at)
+                rows = w2_words.rearrange("e s p b -> p (e s) b")
+                nc.sync.dma_start(out=second_words[:].bitcast(I32), in_=rows.bitcast(I32))
+
+        slot_words, slot_scales = {}, {}
+
+        def gather(n):
+            pair, s = divmod(n, PASSES)
+            if n < FREE_GATHERS:
+                words = keep.tile([P, PAIR], U32, name="words%d" % n, align_bytes=64)
+                scales = keep.tile([P, PAIR], U8, name="scales%d" % n, align_bytes=64)
+            else:
+                at = (n - FREE_GATHERS) * RELU_BYTES
+                words = shared.tile([P, PAIR], U32, name="words%d" % n, align_bytes=64, offset=at)
+                scales = shared.tile([P, PAIR], U8, name="scales%d" % n, align_bytes=64, offset=at + PAIR * 4)
+            offsets = entries(offs_sb, pair * PAIR, PAIR)
+            nc.vector.tensor_copy(scales[:], x_plane[:, s, :].indirect(offsets))
+            nc.vector.tensor_copy(words[:], x_sb[:, s, :].bitcast(U32).indirect(offsets))
+            for i in range(2):
+                slot_words[2 * pair + i, s] = words[:, i * C : (i + 1) * C]
+                slot_scales[2 * pair + i, s] = scales[:, i * C : (i + 1) * C]
+
+        for n in range(FREE_GATHERS):
+            gather(n)
 
         gate_sb = keep.tile([P, E * C], F32, name="gate_sb")
         for u in range(GATE_ROW // 4):
-            spread = psum.tile([P, 4, P], F32, name="spread", tag="b%d" % u, bufs=1)
+            spread = psum.tile([P, 4, P], F32, name="spread", tag="y%d" % u)
             for j in range(4):
                 column = gate_row[:, 4 * u + j : 4 * u + j + 1].to_broadcast([P, P])
                 nc.tensor.transpose(spread[:, j, :], column, identity[:])
@@ -93,85 +133,8 @@ def tile_moe_two_glu_relu_kernel(
                 spread[:].rearrange("m j p -> m p j"),
             )
 
-        weights = shared.tile([P, E * EXPERT_BYTES], U8, name="weights", align_bytes=64, offset=0)
-
-        def first_words(experts, m):
-            at = m * E * FIRST_BYTES
-            part = weights[:, at + experts.start * FIRST_BYTES : at + experts.stop * FIRST_BYTES]
-            return part.rearrange("p (g b) -> p g b", b=2 * H)
-
-        def second_words(experts):
-            at = 2 * E * FIRST_BYTES
-            part = weights[:, at + experts.start * SECOND_BYTES : at + experts.stop * SECOND_BYTES]
-            return part.rearrange("p (e b) -> p e b", b=SECOND_BYTES)
-
-        def load_first_scales(b, m):
-            load_scale_rows(nc.sync, first_planes[b, m], scale_rows((w1_scales, w3_scales)[m], BATCHES[b]))
-
-        def load_first_words(experts, m):
-            rows = (w1_words, w3_words)[m][experts.start : experts.stop].rearrange("e s p b -> p (e s) b")
-            nc.sync.dma_start(out=first_words(experts, m).bitcast(I32), in_=rows.bitcast(I32))
-
-        def load_second_words(experts):
-            rows = w2_words[experts.start : experts.stop].rearrange("e s p b -> p (e s) b")
-            nc.sync.dma_start(out=second_words(experts).bitcast(I32), in_=rows.bitcast(I32))
-
-        for m in range(2):
-            load_first_scales(0, m)
-            load_first_words(LOADS[0], m)
-
-        both = {}
-
-        def gather_scales(b, tile):
-            nc.vector.tensor_copy(tile[:], x_plane[:].indirect(entries(offs_sb, BATCHES[b])))
-            for r in range(4):
-                nc.sync.dma_start(out=moved[b][r:P:32, :].bitcast(I32), in_=tile[16 + r : P : 32, :].bitcast(I32))
-            both[b] = tile
-
-        gather_scales(0, keep.tile([P, len(BATCHES[0]) * C], U8, name="both0", align_bytes=64))
-
-        slot_words = {}
-
-        def over_slots(shape, dtype, name, e, at):
-            return shared.tile(shape, dtype, name=name, align_bytes=64, offset=SLOTS_AT + e * SLOT_BYTES + at)
-
-        def gather_words(s, experts, tile):
-            nc.vector.tensor_copy(tile[:], x_sb[s][:].bitcast(U32).indirect(entries(offs_sb, experts)))
-            for i, e in enumerate(experts):
-                slot_words[e, s] = tile[:, i * C : (i + 1) * C]
-
-        def gather_second_pass(e):
-            gather_words(1, range(e, e + 1), over_slots([P, C], U32, "words%d" % e, e, WORD_BYTES // 2))
-
-        for b, batch in enumerate(BATCHES):
-            gather_words(0, batch, keep.tile([P, len(batch) * C], U32, name="batch%d" % b, align_bytes=64))
-            for e in batch:
-                gather_second_pass(e)
-
-        def load_late_scales(m):
-            first_planes[1, m] = shared.tile(
-                [P, len(BATCHES[1]) * PASSES, H], U8, name="late%d" % m, align_bytes=64, offset=X_AT + m * T * 4
-            )
-            load_first_scales(1, m)
-
-        def load_step(experts):
-            load_first_words(experts, 0)
-            if experts.stop == BATCHES[1].start:
-                load_late_scales(0)
-            if experts.start == BATCHES[1].start:
-                load_late_scales(1)
-            load_first_words(experts, 1)
-            if 2 in experts:
-                load_scale_rows(nc.sync, w2_plane, scale_rows(w2_scales, range(E)))
-                load_second_words(BATCHES[0])
-            if experts.start == BATCHES[1].start:
-                load_second_words(BATCHES[1])
-
-        for experts in LOADS[1:3]:
-            load_step(experts)
-
-        windows = [keep.tile([P, T], F32, name="window%d" % half) for half in range(HALVES)]
-        banks, rectified, hidden, grouped, quantised, results, staged = {}, {}, {}, {}, {}, {}, {}
+        banks, rectified, hidden, quantised = {}, {}, {}, {}
+        staged = [keep.tile([P, E * C], F32, name="staged%d" % half) for half in range(HALVES)]
 
         def woven(bank):
             return bank[:].rearrange("c (p u v) -> c u p v", u=2, v=2)
@@ -179,20 +142,20 @@ def tile_moe_two_glu_relu_kernel(
         def split(tile):
             return tile[:].rearrange("c (u p v) -> c u p v", u=2, v=2)
 
+        def first_scales(e, m, s):
+            if e in EARLY:
+                return early[m][:, e * PASSES + s, :]
+            return late[m][:, (e - LATE.start) * PASSES + s, :]
+
         def first_layer(e, m):
-            b = [e in batch for batch in BATCHES].index(True)
-            if m == 0:
-                tag = "spare" if e == 2 else "turn%d" % (e % 2)
-            else:
-                tag = "b1" if e == 1 else "b0"
-            bank = psum.tile([P, H], F32, name="sums", tag=tag, bufs=1)
+            bank = psum.tile([P, H], F32, name="sums", tag="a" if m == 0 else "b%d" % (e % 2))
             for s in range(PASSES):
                 nc.tensor.matmul_mx(
                     out=bank[:],
                     lhsT=slot_words[e, s].bitcast(FP8X4),
-                    lhsT_scale=(both, moved)[s][b][:, (e - BATCHES[b].start) * C : (e - BATCHES[b].start + 1) * C],
-                    rhs=first_words(range(e, e + 1), m)[:, s, :].bitcast(FP4X4),
-                    rhs_scale=first_planes[b, m][:, (e - BATCHES[b].start) * PASSES + s, :],
+                    lhsT_scale=slot_scales[e, s],
+                    rhs=first_words[e, m][:, s, :].bitcast(FP4X4),
+                    rhs_scale=first_scales(e, m, s),
                     start=(s == 0),
                     stop=(s == PASSES - 1),
                 )
@@ -200,83 +163,67 @@ def tile_moe_two_glu_relu_kernel(
 
         def rectify(e):
             first_layer(e, 0)
-            if e == 0:
-                rectified[e] = over_slots([P, H], F32, "first_relu", E, 0)
-            else:
-                rectified[e] = work.tile([P, H], F32, name="relu_a", align_bytes=64)
+            rectified[e] = shared.tile([P, H], F32, name="relu%d" % e, align_bytes=64, offset=e * RELU_BYTES)
             nc.scalar.activation(split(rectified[e]), woven(banks[e, 0]), RELU)
 
         def product(e):
-            hidden[e] = keep.tile([P, H], BF16, name="h", tag="h%d" % (e % 2), align_bytes=64)
+            hidden[e] = work.tile([P, H], BF16, name="h", align_bytes=64)
             nc.vector.tensor_tensor(split(hidden[e]), woven(banks[e, 1]), split(rectified[e]), MULT)
 
-        def turn(e):
-            turned = psum.tile([P, 2, C], F32, name="turned", tag="turn%d" % (e % 2), bufs=1)
+        def turn_and_quantise(e):
+            turned = psum.tile([P, 2, C], F32, name="turned", tag="turn%d" % (e % 2))
             pairs = hidden[e][:].bitcast(F32)
             for u in range(2):
                 nc.tensor.transpose(turned[:, u, :], pairs[:, u * P : (u + 1) * P], identity[:])
-            grouped[e] = work.tile([P, C * 4], BF16, name="grouped", align_bytes=64)
+            grouped = work.tile([P, C * 4], BF16, name="grouped", align_bytes=64)
             nc.scalar.copy(
-                grouped[e][:].bitcast(F32).rearrange("p (c u) -> p c u", u=2), turned[:].rearrange("p u c -> p c u")
+                grouped[:].bitcast(F32).rearrange("p (c u) -> p c u", u=2), turned[:].rearrange("p u c -> p c u")
             )
-
-        def quantise(e):
             codes = work.tile([P, C], U32, name="codes", align_bytes=64)
             plane = work.tile([P, C], U8, name="h_plane", align_bytes=64)
-            nc.vector.quantize_mx(out=codes[:].bitcast(FP8X4), scales=plane[:], in_=grouped[e][:])
+            nc.vector.quantize_mx(out=codes[:].bitcast(FP8X4), scales=plane[:], in_=grouped[:])
             quantised[e] = (codes, plane)
 
         def second_layer(e):
             codes, plane = quantised[e]
-            bank = psum.tile([P, HALVES, C], F32, name="y_bank", bufs=1)
+            slots = slice(e * C, (e + 1) * C)
             for half in range(HALVES):
+                bank = psum.tile([P, C], F32, name="y_bank", tag="y%d" % half)
                 nc.tensor.matmul_mx(
-                    out=bank[:, half, :],
-                    lhsT=second_words(range(e, e + 1))[:, 0, half * 2 * P : (half + 1) * 2 * P].bitcast(FP4X4),
+                    out=bank[:],
+                    lhsT=second_words[:, e, half * 2 * P : (half + 1) * 2 * P].bitcast(FP4X4),
                     lhsT_scale=w2_plane[:, e, half * P : (half + 1) * P],
                     rhs=codes[:].bitcast(FP8X4),
                     rhs_scale=plane[:],
                     start=True,
                     stop=True,
                 )
-            if e + 2 < E:
-                staged[e] = over_slots([P, HALVES, C], F32, "y%d" % e, e + 2, 0)
-            else:
-                staged[e] = keep.tile([P, HALVES, C], F32, name="y", tag="h%d" % ((e + 1) % 2), align_bytes=64)
-            nc.scalar.copy(staged[e][:], bank[:])
+                if half == 0:
+                    nc.scalar.copy(staged[0][:, slots], bank[:])
+                else:
+                    nc.vector.tensor_tensor(staged[1][:, slots], bank[:], gate_sb[:, slots], MULT)
 
-        def scatter(e):
-            for half in range(HALVES):
-                nc.vector.tensor_tensor(
-                    windows[half][:].indirect(entries(dst_sb, range(e, e + 1))),
-                    staged[e][:, half, :],
-                    gate_sb[:, e * C : (e + 1) * C],
-                    MULT,
-                )
-
-        for e in range(2):
-            rectify(e)
+        rectify(0)
+        for e in range(E):
             first_layer(e, 1)
-        product(0)
-        gather_scales(1, over_slots([P, len(BATCHES[1]) * C], U8, "both1", E, 0))
-        product(1)
-        for experts in LOADS[3:]:
-            load_step(experts)
-        rectify(2)
-        turn(0)
-        quantise(0)
-        for e in range(1, E + 1):
-            if e < E:
-                turn(e)
             if e + 1 < E:
-                first_layer(e + 1, 1)
-            second_layer(e - 1)
-            if e + 2 < E:
-                rectify(e + 2)
-            if e + 1 < E:
-                product(e + 1)
-            if e < E:
-                quantise(e)
-            scatter(e - 1)
+                rectify(e + 1)
+            product(e)
+            if e + FREE_GATHERS < E:
+                gather(e + FREE_GATHERS)
+            if e > 0:
+                second_layer(e - 1)
+            turn_and_quantise(e)
+        second_layer(E - 1)
+
+        windows = [
+            shared.tile([P, T], F32, name="window%d" % half, align_bytes=64, offset=WINDOWS_AT + half * T * 4)
+            for half in range(HALVES)
+        ]
+        for first in range(0, E * C, PAIR):
+            slots = slice(first, first + PAIR)
+            offsets = entries(dst_sb, first, PAIR)
+            nc.vector.tensor_tensor(windows[0][:].indirect(offsets), staged[0][:, slots], gate_sb[:, slots], MULT)
+            nc.scalar.activation(windows[1][:].indirect(offsets), staged[1][:, slots], COPY)
         for half in range(HALVES):
             nc.sync.dma_start(out=out[half * P : (half + 1) * P, :], in_=windows[half][:])

@@ -25,10 +25,14 @@ GATE_ROW = E * C // P
 PAIR = 2 * C
 EARLY = range(0, 4)
 LATE = range(4, E)
-RELU_BYTES = H * 4
-WINDOWS_AT = E * RELU_BYTES
-LOADS = [range(0, 1), range(1, 3), range(3, 5), range(5, 8)]
-FREE_GATHERS = 4
+FREE_GATHERS = 6
+REGION = 3072
+STAGED_AT, RELU_AT, CODES_AT, PLANE_AT, SCALES_AT, WORDS_AT = 0, 960, 1024, 1536, 1664, 1920
+FIRST_BYTES = PASSES * 2 * H
+W3_AT = E * REGION + FIRST_BYTES
+SHARED = (2, 3, 4, 5, 6, 7)
+LATE_AT = W3_AT - FIRST_BYTES
+GROUPED_AT = W3_AT + (E + 2) * FIRST_BYTES
 
 
 def load_scale_rows(queue, plane, rows, which=range(4)):
@@ -58,69 +62,84 @@ def tile_moe_two_glu_relu_kernel(
         def entries(lists, first, count):
             return lists[:, first // 16 : (first + count) // 16]
 
+        def behind_product(e, shape, dtype, name, at):
+            if e is None or e >= E:
+                return keep.tile(shape, dtype, name=name, align_bytes=64)
+            return shared.tile(shape, dtype, name=name, align_bytes=64, offset=e * REGION + at)
+
         x_plane = keep.tile([P, PASSES, T], U8, name="x_plane", align_bytes=64)
         nc.gpsimd.memset(x_plane[:].bitcast(I32), 0)
-        early = [zeroed("early%d" % m, [P, len(EARLY) * PASSES, H]) for m in range(2)]
-        w2_plane = zeroed("w2_plane", [P, E, N])
-        late = [zeroed("late%d" % m, [P, len(LATE) * PASSES, H]) for m in range(2)]
+        early, late = {}, {}
+        for m in range(2):
+            early[m] = zeroed("early%d" % m, [P, len(EARLY) * PASSES, H])
+            late[m] = zeroed("late%d" % m, [P, len(LATE) * PASSES, H])
         identity = keep.tile([P, P], F32, name="identity")
         make_identity(nc, identity[:])
 
         offs_sb = keep.tile([P, T // 16], U16, name="offs_sb")
         nc.sync.dma_start(offs_sb[:], offs)
-        dst_sb = keep.tile([P, T // 16], U16, name="dst_sb")
-        nc.sync.dma_start(dst_sb[:], dst)
+        gate_row = keep.tile([P, GATE_ROW], F32, name="gate_row")
+        nc.sync.dma_start(out=gate_row[:], in_=gate[0].rearrange("(p j) -> p j", j=GATE_ROW))
         load_scale_rows(nc.sync, x_plane, x_scales)
         load_scale_rows(nc.sync, early[0], scale_rows(w1_scales, EARLY), range(0, 1))
         x_sb = keep.tile([P, PASSES, T], I32, name="x_sb", align_bytes=64)
         nc.sync.dma_start(out=x_sb[:], in_=x_words.rearrange("s p t r -> p s (t r)").bitcast(I32))
         load_scale_rows(nc.sync, early[0], scale_rows(w1_scales, EARLY), range(1, 4))
         load_scale_rows(nc.sync, early[1], scale_rows(w3_scales, EARLY))
-        gate_row = keep.tile([P, GATE_ROW], F32, name="gate_row")
-        nc.gpsimd.dma_start(out=gate_row[:], in_=gate[0].rearrange("(p j) -> p j", j=GATE_ROW))
-        load_scale_rows(nc.gpsimd, w2_plane, scale_rows(w2_scales, range(E)))
         for m in range(2):
             load_scale_rows(nc.gpsimd, late[m], scale_rows((w1_scales, w3_scales)[m], LATE))
 
-        first_words = {}
+        first_words, second_words = {}, {}
 
         def load_first(experts, m):
             name = "w%d_%d" % (2 * m + 1, experts.start)
-            tile = keep.tile([P, len(experts) * PASSES, 2 * H], U8, name=name, align_bytes=64)
+            if m == 0 and experts.start == 0:
+                tile = shared.tile([P, PASSES, 2 * H], U8, name=name, align_bytes=64, offset=LATE_AT)
+            elif m == 0:
+                tile = keep.tile([P, len(experts) * PASSES, 2 * H], U8, name=name, align_bytes=64)
+            else:
+                at = W3_AT + experts.start * FIRST_BYTES
+                tile = shared.tile([P, PASSES, 2 * H], U8, name=name, align_bytes=64, offset=at)
             rows = (w1_words, w3_words)[m][experts.start : experts.stop].rearrange("e s p b -> p (e s) b")
             nc.sync.dma_start(out=tile[:].bitcast(I32), in_=rows.bitcast(I32))
             for i, e in enumerate(experts):
                 first_words[e, m] = tile[:, i * PASSES : (i + 1) * PASSES, :]
 
-        for experts in LOADS:
-            for m in range(2):
-                load_first(experts, m)
-            if 2 in experts:
-                at = WINDOWS_AT + T * 2
-                second_words = shared.tile([P, E, 2 * N], U8, name="w2", align_bytes=64, offset=at)
-                rows = w2_words.rearrange("e s p b -> p (e s) b")
-                nc.sync.dma_start(out=second_words[:].bitcast(I32), in_=rows.bitcast(I32))
+        def load_second(experts):
+            tile = keep.tile([P, len(experts), 2 * N], U8, name="w2_%d" % experts.start, align_bytes=64)
+            rows = w2_words[experts.start : experts.stop].rearrange("e s p b -> p (e s) b")
+            nc.sync.dma_start(out=tile[:].bitcast(I32), in_=rows.bitcast(I32))
+            for i, e in enumerate(experts):
+                second_words[e] = tile[:, i, :]
+
+        def load_experts(experts):
+            for e in experts:
+                for m in range(2):
+                    load_first(range(e, e + 1), m)
+                if e == LATE.start:
+                    load_second(LATE)
+
+        load_experts(range(0, 3))
+        load_first(range(3, 4), 0)
 
         slot_words, slot_scales = {}, {}
 
-        def gather(n):
+        def gather_scales(n, scales):
             pair, s = divmod(n, PASSES)
-            if n < FREE_GATHERS:
-                words = keep.tile([P, PAIR], U32, name="words%d" % n, align_bytes=64)
-                scales = keep.tile([P, PAIR], U8, name="scales%d" % n, align_bytes=64)
-            else:
-                at = (n - FREE_GATHERS) * RELU_BYTES
-                words = shared.tile([P, PAIR], U32, name="words%d" % n, align_bytes=64, offset=at)
-                scales = shared.tile([P, PAIR], U8, name="scales%d" % n, align_bytes=64, offset=at + PAIR * 4)
-            offsets = entries(offs_sb, pair * PAIR, PAIR)
-            nc.vector.tensor_copy(scales[:], x_plane[:, s, :].indirect(offsets))
-            nc.vector.tensor_copy(words[:], x_sb[:, s, :].bitcast(U32).indirect(offsets))
+            nc.vector.tensor_copy(scales[:], x_plane[:, s, :].indirect(entries(offs_sb, pair * PAIR, PAIR)))
             for i in range(2):
-                slot_words[2 * pair + i, s] = words[:, i * C : (i + 1) * C]
                 slot_scales[2 * pair + i, s] = scales[:, i * C : (i + 1) * C]
 
+        def gather_words(n, behind):
+            pair, s = divmod(n, PASSES)
+            words = behind_product(behind, [P, PAIR], U32, "words%d" % n, WORDS_AT)
+            nc.vector.tensor_copy(words[:], x_sb[:, s, :].bitcast(U32).indirect(entries(offs_sb, pair * PAIR, PAIR)))
+            for i in range(2):
+                slot_words[2 * pair + i, s] = words[:, i * C : (i + 1) * C]
+
         for n in range(FREE_GATHERS):
-            gather(n)
+            gather_scales(n, behind_product(None, [P, PAIR], U8, "scales%d" % n, 0))
+            gather_words(n, None)
 
         gate_sb = keep.tile([P, E * C], F32, name="gate_sb")
         for u in range(GATE_ROW // 4):
@@ -133,8 +152,8 @@ def tile_moe_two_glu_relu_kernel(
                 spread[:].rearrange("m j p -> m p j"),
             )
 
-        banks, rectified, hidden, quantised = {}, {}, {}, {}
-        staged = [keep.tile([P, E * C], F32, name="staged%d" % half) for half in range(HALVES)]
+        banks, rectified, hidden, grouped, quantised, results, staged = {}, {}, {}, {}, {}, {}, {}
+        windows = [keep.tile([P, T], F32, name="window%d" % half) for half in range(HALVES)]
 
         def woven(bank):
             return bank[:].rearrange("c (p u v) -> c u p v", u=2, v=2)
@@ -142,20 +161,16 @@ def tile_moe_two_glu_relu_kernel(
         def split(tile):
             return tile[:].rearrange("c (u p v) -> c u p v", u=2, v=2)
 
-        def first_scales(e, m, s):
-            if e in EARLY:
-                return early[m][:, e * PASSES + s, :]
-            return late[m][:, (e - LATE.start) * PASSES + s, :]
-
         def first_layer(e, m):
             bank = psum.tile([P, H], F32, name="sums", tag="a" if m == 0 else "b%d" % (e % 2))
+            plane, first = (early[m], EARLY.start) if e in EARLY else (late[m], LATE.start)
             for s in range(PASSES):
                 nc.tensor.matmul_mx(
                     out=bank[:],
                     lhsT=slot_words[e, s].bitcast(FP8X4),
                     lhsT_scale=slot_scales[e, s],
                     rhs=first_words[e, m][:, s, :].bitcast(FP4X4),
-                    rhs_scale=first_scales(e, m, s),
+                    rhs_scale=plane[:, (e - first) * PASSES + s, :],
                     start=(s == 0),
                     stop=(s == PASSES - 1),
                 )
@@ -163,67 +178,96 @@ def tile_moe_two_glu_relu_kernel(
 
         def rectify(e):
             first_layer(e, 0)
-            rectified[e] = shared.tile([P, H], F32, name="relu%d" % e, align_bytes=64, offset=e * RELU_BYTES)
+            rectified[e] = behind_product(e, [P, H], F32, "relu%d" % e, RELU_AT)
             nc.scalar.activation(split(rectified[e]), woven(banks[e, 0]), RELU)
 
         def product(e):
-            hidden[e] = work.tile([P, H], BF16, name="h", align_bytes=64)
+            at = W3_AT + (e + 1 if e > 0 else E + 1) * FIRST_BYTES
+            hidden[e] = shared.tile([P, H], BF16, name="h%d" % e, align_bytes=64, offset=at)
             nc.vector.tensor_tensor(split(hidden[e]), woven(banks[e, 1]), split(rectified[e]), MULT)
 
-        def turn_and_quantise(e):
+        def turn(e):
             turned = psum.tile([P, 2, C], F32, name="turned", tag="turn%d" % (e % 2))
             pairs = hidden[e][:].bitcast(F32)
             for u in range(2):
                 nc.tensor.transpose(turned[:, u, :], pairs[:, u * P : (u + 1) * P], identity[:])
-            grouped = work.tile([P, C * 4], BF16, name="grouped", align_bytes=64)
+            if e == 0:
+                grouped[e] = shared.tile([P, C * 4], BF16, name="grouped0", align_bytes=64, offset=GROUPED_AT)
+            else:
+                grouped[e] = work.tile([P, C * 4], BF16, name="grouped", align_bytes=64)
             nc.scalar.copy(
-                grouped[:].bitcast(F32).rearrange("p (c u) -> p c u", u=2), turned[:].rearrange("p u c -> p c u")
+                grouped[e][:].bitcast(F32).rearrange("p (c u) -> p c u", u=2), turned[:].rearrange("p u c -> p c u")
             )
-            codes = work.tile([P, C], U32, name="codes", align_bytes=64)
-            plane = work.tile([P, C], U8, name="h_plane", align_bytes=64)
-            nc.vector.quantize_mx(out=codes[:].bitcast(FP8X4), scales=plane[:], in_=grouped[:])
+
+        def quantise(e, behind):
+            codes = behind_product(behind, [P, C], U32, "codes%d" % e, CODES_AT)
+            plane = behind_product(behind, [P, C], U8, "h_plane%d" % e, PLANE_AT)
+            nc.vector.quantize_mx(out=codes[:].bitcast(FP8X4), scales=plane[:], in_=grouped[e][:])
             quantised[e] = (codes, plane)
 
         def second_layer(e):
             codes, plane = quantised[e]
-            slots = slice(e * C, (e + 1) * C)
+            results[e] = psum.tile([P, HALVES, C], F32, name="y_bank", tag="y%d" % (e % 2))
             for half in range(HALVES):
-                bank = psum.tile([P, C], F32, name="y_bank", tag="y%d" % half)
                 nc.tensor.matmul_mx(
-                    out=bank[:],
-                    lhsT=second_words[:, e, half * 2 * P : (half + 1) * 2 * P].bitcast(FP4X4),
+                    out=results[e][:, half, :],
+                    lhsT=second_words[e][:, half * 2 * P : (half + 1) * 2 * P].bitcast(FP4X4),
                     lhsT_scale=w2_plane[:, e, half * P : (half + 1) * P],
                     rhs=codes[:].bitcast(FP8X4),
                     rhs_scale=plane[:],
                     start=True,
                     stop=True,
                 )
-                if half == 0:
-                    nc.scalar.copy(staged[0][:, slots], bank[:])
-                else:
-                    nc.vector.tensor_tensor(staged[1][:, slots], bank[:], gate_sb[:, slots], MULT)
+
+        def weigh(e, behind):
+            staged[e] = behind_product(behind, [P, HALVES, C], F32, "staged%d" % e, STAGED_AT)
+            weights = gate_sb[:, e * C : (e + 1) * C].unsqueeze(1).to_broadcast([P, HALVES, C])
+            nc.vector.tensor_tensor(staged[e][:], results[e][:], weights, MULT)
+
+        def scatter(e):
+            offsets = entries(dst_sb, e * C, C)
+            nc.scalar.activation(windows[1][:].indirect(offsets), staged[e][:, 1, :], COPY)
+            if e in SHARED:
+                nc.vector.tensor_copy(windows[0][:].indirect(offsets), staged[e][:, 0, :])
+            else:
+                nc.scalar.activation(windows[0][:].indirect(offsets), staged[e][:, 0, :], COPY)
 
         rectify(0)
-        for e in range(E):
-            first_layer(e, 1)
-            if e + 1 < E:
-                rectify(e + 1)
-            product(e)
-            if e + FREE_GATHERS < E:
-                gather(e + FREE_GATHERS)
-            if e > 0:
-                second_layer(e - 1)
-            turn_and_quantise(e)
-        second_layer(E - 1)
-
-        windows = [
-            shared.tile([P, T], F32, name="window%d" % half, align_bytes=64, offset=WINDOWS_AT + half * T * 4)
-            for half in range(HALVES)
-        ]
-        for first in range(0, E * C, PAIR):
-            slots = slice(first, first + PAIR)
-            offsets = entries(dst_sb, first, PAIR)
-            nc.vector.tensor_tensor(windows[0][:].indirect(offsets), staged[0][:, slots], gate_sb[:, slots], MULT)
-            nc.scalar.activation(windows[1][:].indirect(offsets), staged[1][:, slots], COPY)
+        w2_plane = shared.tile([P, E, N], U8, name="w2_plane", align_bytes=64, offset=LATE_AT)
+        load_scale_rows(nc.sync, w2_plane, scale_rows(w2_scales, range(E)))
+        load_second(EARLY)
+        dst_sb = keep.tile([P, T // 16], U16, name="dst_sb")
+        nc.sync.dma_start(dst_sb[:], dst)
+        load_first(range(3, 4), 1)
+        load_experts(range(4, E))
+        for step in range(E + 2):
+            if step < E:
+                first_layer(step, 1)
+            if step + 1 < E:
+                rectify(step + 1)
+            if step < E:
+                product(step)
+            if step == 1:
+                weigh(0, step)
+                scatter(0)
+            if step >= 3:
+                weigh(step - 2, step)
+            if 2 <= step <= E:
+                quantise(step - 1, step)
+            if step >= 3:
+                scatter(step - 2)
+            if step == 0:
+                gather_scales(6, behind_product(0, [P, PAIR], U8, "scales6", SCALES_AT))
+                gather_words(6, 0)
+            if step == 1:
+                gather_words(7, 1)
+            if step < E:
+                turn(step)
+            if step == 0:
+                quantise(0, None)
+                gather_scales(7, shared.tile([P, PAIR], U8, name="scales7", align_bytes=64, offset=GROUPED_AT))
+                second_layer(0)
+            if 2 <= step <= E:
+                second_layer(step - 1)
         for half in range(HALVES):
             nc.sync.dma_start(out=out[half * P : (half + 1) * P, :], in_=windows[half][:])

@@ -22,22 +22,20 @@ P = 128
 PASSES = K // 512
 HALVES = N // P
 GATE_ROW = E * C // P
-PAIR = 2 * C
 EARLY = range(0, 4)
 LATE = range(4, E)
-FREE_GATHERS = 6
-REGION = 3072
-STAGED_AT, RELU_AT, CODES_AT, PLANE_AT, SCALES_AT, WORDS_AT = 0, 960, 1024, 1536, 1664, 1920
+WORD_GATHERS = [range(0, 2), range(2, 4), range(4, 8)]
+STAGED_AT, CODES_AT = 0, 1024
 FIRST_BYTES = PASSES * 2 * H
-W3_AT = E * REGION + FIRST_BYTES
-SHARED = (2, 3, 4, 5, 6, 7)
-LATE_AT = W3_AT - FIRST_BYTES
-GROUPED_AT = W3_AT + (E + 2) * FIRST_BYTES
+W1_AT = 0
+W3_AT = W1_AT + E * FIRST_BYTES
+X_AT = W3_AT + E * FIRST_BYTES
+VECTOR_HALF = {1: 0, 2: 0, 3: 0, 4: 0, 5: 1, 7: 0}
 
 
-def load_scale_rows(queue, plane, rows, which=range(4)):
+def load_scale_rows(queue, plane, rows):
     by_r = rows.rearrange("g (q r) n -> r q g n", r=4)
-    for r in which:
+    for r in range(4):
         queue.dma_start(out=plane[r:P:32, :, :].bitcast(I32), in_=by_r[r].bitcast(I32))
 
 
@@ -65,81 +63,78 @@ def tile_moe_two_glu_relu_kernel(
         def behind_product(e, shape, dtype, name, at):
             if e is None or e >= E:
                 return keep.tile(shape, dtype, name=name, align_bytes=64)
-            return shared.tile(shape, dtype, name=name, align_bytes=64, offset=e * REGION + at)
+            return shared.tile(shape, dtype, name=name, align_bytes=64, offset=W3_AT + e * FIRST_BYTES + at)
 
-        x_plane = keep.tile([P, PASSES, T], U8, name="x_plane", align_bytes=64)
-        nc.gpsimd.memset(x_plane[:].bitcast(I32), 0)
-        early, late = {}, {}
-        for m in range(2):
-            early[m] = zeroed("early%d" % m, [P, len(EARLY) * PASSES, H])
-            late[m] = zeroed("late%d" % m, [P, len(LATE) * PASSES, H])
+        x_plane = zeroed("x_plane", [P, T])
+        early = [zeroed("early%d" % m, [P, len(EARLY) * PASSES, H]) for m in range(2)]
+        moved = zeroed("moved", [P, E * C])
+        late = {}
         identity = keep.tile([P, P], F32, name="identity")
-        make_identity(nc, identity[:])
-
-        offs_sb = keep.tile([P, T // 16], U16, name="offs_sb")
-        nc.sync.dma_start(offs_sb[:], offs)
-        gate_row = keep.tile([P, GATE_ROW], F32, name="gate_row")
-        nc.sync.dma_start(out=gate_row[:], in_=gate[0].rearrange("(p j) -> p j", j=GATE_ROW))
-        load_scale_rows(nc.sync, x_plane, x_scales)
-        load_scale_rows(nc.sync, early[0], scale_rows(w1_scales, EARLY), range(0, 1))
-        x_sb = keep.tile([P, PASSES, T], I32, name="x_sb", align_bytes=64)
-        nc.sync.dma_start(out=x_sb[:], in_=x_words.rearrange("s p t r -> p s (t r)").bitcast(I32))
-        load_scale_rows(nc.sync, early[0], scale_rows(w1_scales, EARLY), range(1, 4))
-        load_scale_rows(nc.sync, early[1], scale_rows(w3_scales, EARLY))
-        for m in range(2):
-            load_scale_rows(nc.gpsimd, late[m], scale_rows((w1_scales, w3_scales)[m], LATE))
+        nc.vector.memset(identity[:], 0.0)
+        make_identity(nc, identity[:], nomemset=True)
 
         first_words, second_words = {}, {}
 
-        def load_first(experts, m):
-            name = "w%d_%d" % (2 * m + 1, experts.start)
-            if m == 0 and experts.start == 0:
-                tile = shared.tile([P, PASSES, 2 * H], U8, name=name, align_bytes=64, offset=LATE_AT)
-            elif m == 0:
-                tile = keep.tile([P, len(experts) * PASSES, 2 * H], U8, name=name, align_bytes=64)
-            else:
-                at = W3_AT + experts.start * FIRST_BYTES
-                tile = shared.tile([P, PASSES, 2 * H], U8, name=name, align_bytes=64, offset=at)
-            rows = (w1_words, w3_words)[m][experts.start : experts.stop].rearrange("e s p b -> p (e s) b")
-            nc.sync.dma_start(out=tile[:].bitcast(I32), in_=rows.bitcast(I32))
-            for i, e in enumerate(experts):
-                first_words[e, m] = tile[:, i * PASSES : (i + 1) * PASSES, :]
+        def load_first(e, m):
+            at = (W1_AT, W3_AT)[m] + e * FIRST_BYTES
+            name = "w%d_%d" % (2 * m + 1, e)
+            first_words[e, m] = shared.tile([P, PASSES, 2 * H], U8, name=name, align_bytes=64, offset=at)
+            rows = (w1_words, w3_words)[m][e].rearrange("s p b -> p s b")
+            nc.sync.dma_start(out=first_words[e, m][:].bitcast(I32), in_=rows.bitcast(I32))
+
+        offs_sb = keep.tile([P, T // 16], U16, name="offs_sb")
+        nc.sync.dma_start(offs_sb[:], offs)
+        load_first(0, 0)
+        gate_row = keep.tile([P, GATE_ROW], F32, name="gate_row")
+        nc.sync.dma_start(out=gate_row[:], in_=gate[0].rearrange("(p j) -> p j", j=GATE_ROW))
+        x_rows = x_scales.rearrange("s (q r) t -> r q s t", r=4)
+        for r in range(4):
+            nc.sync.dma_start(out=x_plane[r:P:16, :].bitcast(I32), in_=x_rows[r].bitcast(I32))
+        x_sb = shared.tile([P, PASSES, T], I32, name="x_sb", align_bytes=64, offset=X_AT)
+        nc.sync.dma_start(out=x_sb[:], in_=x_words.rearrange("s p t r -> p s (t r)").bitcast(I32))
+        for m in range(2):
+            load_scale_rows(nc.sync, early[m], scale_rows((w1_scales, w3_scales)[m], EARLY))
+
+        both = keep.tile([P, E * C], U8, name="both", align_bytes=64)
+        for first in range(0, E * C, T // 2):
+            nc.vector.tensor_copy(both[:, first : first + T // 2], x_plane[:].indirect(entries(offs_sb, first, T // 2)))
+
+
+        def load_late_rows(m):
+            at = X_AT + m * T * 4
+            late[m] = shared.tile([P, len(LATE) * PASSES, H], U8, name="late%d" % m, align_bytes=64, offset=at)
+            load_scale_rows(nc.sync, late[m], scale_rows((w1_scales, w3_scales)[m], LATE))
 
         def load_second(experts):
             tile = keep.tile([P, len(experts), 2 * N], U8, name="w2_%d" % experts.start, align_bytes=64)
-            rows = w2_words[experts.start : experts.stop].rearrange("e s p b -> p (e s) b")
-            nc.sync.dma_start(out=tile[:].bitcast(I32), in_=rows.bitcast(I32))
+            rows = w2_words.bitcast(I32)[experts.start : experts.stop].rearrange("e s p b -> p (e s) b")
+            nc.sync.dma_start(out=tile[:].bitcast(I32), in_=rows)
             for i, e in enumerate(experts):
                 second_words[e] = tile[:, i, :]
 
-        def load_experts(experts):
-            for e in experts:
-                for m in range(2):
-                    load_first(range(e, e + 1), m)
-                if e == LATE.start:
-                    load_second(LATE)
+        for r in range(4):
+            nc.sync.dma_start(out=moved[r:P:32, :].bitcast(I32), in_=both[16 + r : P : 32, :].bitcast(I32))
+        load_first(0, 1)
+        for m in range(2):
+            load_first(1, m)
+        for m in range(2):
+            load_first(2, m)
+        load_first(3, 0)
 
-        load_experts(range(0, 3))
-        load_first(range(3, 4), 0)
+        slot_words = {}
 
-        slot_words, slot_scales = {}, {}
+        def gather_words(experts, s, behind):
+            name = "words%d_%d" % (experts.start, s)
+            words = behind_product(behind, [P, len(experts) * C], U32, name, 0)
+            offsets = entries(offs_sb, experts.start * C, len(experts) * C)
+            nc.vector.tensor_copy(words[:], x_sb[:, s, :].bitcast(U32).indirect(offsets))
+            for i, e in enumerate(experts):
+                slot_words[e, s] = words[:, i * C : (i + 1) * C]
 
-        def gather_scales(n, scales):
-            pair, s = divmod(n, PASSES)
-            nc.vector.tensor_copy(scales[:], x_plane[:, s, :].indirect(entries(offs_sb, pair * PAIR, PAIR)))
-            for i in range(2):
-                slot_scales[2 * pair + i, s] = scales[:, i * C : (i + 1) * C]
-
-        def gather_words(n, behind):
-            pair, s = divmod(n, PASSES)
-            words = behind_product(behind, [P, PAIR], U32, "words%d" % n, WORDS_AT)
-            nc.vector.tensor_copy(words[:], x_sb[:, s, :].bitcast(U32).indirect(entries(offs_sb, pair * PAIR, PAIR)))
-            for i in range(2):
-                slot_words[2 * pair + i, s] = words[:, i * C : (i + 1) * C]
-
-        for n in range(FREE_GATHERS):
-            gather_scales(n, behind_product(None, [P, PAIR], U8, "scales%d" % n, 0))
-            gather_words(n, None)
+        for experts in WORD_GATHERS[:-1]:
+            for s in range(PASSES):
+                gather_words(experts, s, None)
+        gather_words(WORD_GATHERS[-1], 0, None)
 
         gate_sb = keep.tile([P, E * C], F32, name="gate_sb")
         for u in range(GATE_ROW // 4):
@@ -168,7 +163,7 @@ def tile_moe_two_glu_relu_kernel(
                 nc.tensor.matmul_mx(
                     out=bank[:],
                     lhsT=slot_words[e, s].bitcast(FP8X4),
-                    lhsT_scale=slot_scales[e, s],
+                    lhsT_scale=(both, moved)[s][:, e * C : (e + 1) * C],
                     rhs=first_words[e, m][:, s, :].bitcast(FP4X4),
                     rhs_scale=plane[:, (e - first) * PASSES + s, :],
                     start=(s == 0),
@@ -178,12 +173,11 @@ def tile_moe_two_glu_relu_kernel(
 
         def rectify(e):
             first_layer(e, 0)
-            rectified[e] = behind_product(e, [P, H], F32, "relu%d" % e, RELU_AT)
+            rectified[e] = work.tile([P, H], F32, name="relu", align_bytes=64)
             nc.scalar.activation(split(rectified[e]), woven(banks[e, 0]), RELU)
 
         def product(e):
-            at = W3_AT + (e + 1 if e > 0 else E + 1) * FIRST_BYTES
-            hidden[e] = shared.tile([P, H], BF16, name="h%d" % e, align_bytes=64, offset=at)
+            hidden[e] = work.tile([P, H], BF16, name="h", align_bytes=64)
             nc.vector.tensor_tensor(split(hidden[e]), woven(banks[e, 1]), split(rectified[e]), MULT)
 
         def turn(e):
@@ -191,17 +185,14 @@ def tile_moe_two_glu_relu_kernel(
             pairs = hidden[e][:].bitcast(F32)
             for u in range(2):
                 nc.tensor.transpose(turned[:, u, :], pairs[:, u * P : (u + 1) * P], identity[:])
-            if e == 0:
-                grouped[e] = shared.tile([P, C * 4], BF16, name="grouped0", align_bytes=64, offset=GROUPED_AT)
-            else:
-                grouped[e] = work.tile([P, C * 4], BF16, name="grouped", align_bytes=64)
+            grouped[e] = work.tile([P, C * 4], BF16, name="grouped", align_bytes=64)
             nc.scalar.copy(
                 grouped[e][:].bitcast(F32).rearrange("p (c u) -> p c u", u=2), turned[:].rearrange("p u c -> p c u")
             )
 
         def quantise(e, behind):
             codes = behind_product(behind, [P, C], U32, "codes%d" % e, CODES_AT)
-            plane = behind_product(behind, [P, C], U8, "h_plane%d" % e, PLANE_AT)
+            plane = keep.tile([P, C], U8, name="h_plane%d" % e, align_bytes=64)
             nc.vector.quantize_mx(out=codes[:].bitcast(FP8X4), scales=plane[:], in_=grouped[e][:])
             quantised[e] = (codes, plane)
 
@@ -226,48 +217,64 @@ def tile_moe_two_glu_relu_kernel(
 
         def scatter(e):
             offsets = entries(dst_sb, e * C, C)
-            nc.scalar.activation(windows[1][:].indirect(offsets), staged[e][:, 1, :], COPY)
-            if e in SHARED:
-                nc.vector.tensor_copy(windows[0][:].indirect(offsets), staged[e][:, 0, :])
-            else:
-                nc.scalar.activation(windows[0][:].indirect(offsets), staged[e][:, 0, :], COPY)
+            for half in range(HALVES):
+                if VECTOR_HALF.get(e) == half:
+                    nc.vector.tensor_copy(windows[half][:].indirect(offsets), staged[e][:, half, :])
+                else:
+                    nc.scalar.activation(windows[half][:].indirect(offsets), staged[e][:, half, :], COPY)
 
         rectify(0)
-        w2_plane = shared.tile([P, E, N], U8, name="w2_plane", align_bytes=64, offset=LATE_AT)
+        w2_plane = shared.tile([P, E, N], U8, name="w2_plane", align_bytes=64, offset=W1_AT)
         load_scale_rows(nc.sync, w2_plane, scale_rows(w2_scales, range(E)))
-        load_second(EARLY)
+        load_second(range(0, 2))
         dst_sb = keep.tile([P, T // 16], U16, name="dst_sb")
         nc.sync.dma_start(dst_sb[:], dst)
-        load_first(range(3, 4), 1)
-        load_experts(range(4, E))
-        for step in range(E + 2):
-            if step < E:
-                first_layer(step, 1)
+        first_layer(0, 1)
+        rectify(1)
+        for step in range(E - 1):
+            product(step)
+            turn(step)
             if step + 1 < E:
-                rectify(step + 1)
-            if step < E:
-                product(step)
+                first_layer(step + 1, 1)
             if step == 1:
-                weigh(0, step)
+                load_late_rows(0)
+                load_first(3, 1)
+                load_first(4, 0)
+                load_late_rows(1)
+                load_second(range(2, 5))
+                for e in LATE:
+                    load_first(e, 1)
+                    if e + 1 < E:
+                        load_first(e + 1, 0)
+                load_second(range(5, 8))
+                weigh(0, None)
                 scatter(0)
             if step >= 3:
                 weigh(step - 2, step)
-            if 2 <= step <= E:
+            if step >= 2:
                 quantise(step - 1, step)
             if step >= 3:
                 scatter(step - 2)
             if step == 0:
-                gather_scales(6, behind_product(0, [P, PAIR], U8, "scales6", SCALES_AT))
-                gather_words(6, 0)
-            if step == 1:
-                gather_words(7, 1)
-            if step < E:
-                turn(step)
-            if step == 0:
+                gather_words(WORD_GATHERS[-1], 1, 0)
                 quantise(0, None)
-                gather_scales(7, shared.tile([P, PAIR], U8, name="scales7", align_bytes=64, offset=GROUPED_AT))
                 second_layer(0)
-            if 2 <= step <= E:
+            if step >= 2:
                 second_layer(step - 1)
+            if step + 2 < E:
+                rectify(step + 2)
+        last = E - 1
+        weigh(last - 2, None)
+        product(last)
+        turn(last)
+        quantise(last - 1, last)
+        second_layer(last - 1)
+        scatter(last - 2)
+        weigh(last - 1, None)
+        quantise(last, None)
+        second_layer(last)
+        scatter(last - 1)
+        weigh(last, None)
+        scatter(last)
         for half in range(HALVES):
             nc.sync.dma_start(out=out[half * P : (half + 1) * P, :], in_=windows[half][:])

from contextlib import ExitStack

import concourse.mybir as mybir
from concourse.masks import make_identity

K, T, E, C, H, N = 1024, 1024, 8, 128, 512, 256
FLOPS = 2 * E * C * (2 * K * H + H * N)

F32 = mybir.dt.float32
BF16 = mybir.dt.bfloat16
I32 = mybir.dt.int32
U32 = mybir.dt.uint32
U16 = mybir.dt.uint16
U8 = mybir.dt.uint8
FP8X4 = mybir.dt.float8_e4m3fn_x4
FP4X4 = mybir.dt.float4_e2m1fn_x4
MULT = mybir.AluOpType.mult
RELU = mybir.ActivationFunctionType.Relu
COPY = mybir.ActivationFunctionType.Copy

P = 128
PASSES = K // 512
HALVES = N // P
GATE_ROW = E * C // P
EARLY = range(0, 4)
LATE = range(4, E)
WORD_GATHERS = [range(0, 2), range(2, 4), range(4, 8)]
STAGED_AT, CODES_AT = 0, 1024
FIRST_BYTES = PASSES * 2 * H
W1_AT = 0
W3_AT = W1_AT + E * FIRST_BYTES
X_AT = W3_AT + E * FIRST_BYTES
VECTOR_HALF = {1: 0, 2: 0, 3: 0, 4: 0, 5: 1, 7: 0}


def load_scale_rows(queue, plane, rows):
    by_r = rows.rearrange("g (q r) n -> r q g n", r=4)
    for r in range(4):
        queue.dma_start(out=plane[r:P:32, :, :].bitcast(I32), in_=by_r[r].bitcast(I32))


def tile_moe_two_glu_relu_kernel(
    tc, x_words, x_scales, w1_words, w1_scales, w3_words, w3_scales, w2_words, w2_scales, gate, offs, dst, out
):
    nc = tc.nc
    with ExitStack() as ctx:
        keep = ctx.enter_context(tc.tile_pool(name="keep", bufs=1))
        shared = ctx.enter_context(tc.tile_pool(name="shared", bufs=1))
        work = ctx.enter_context(tc.tile_pool(name="work", bufs=2))
        psum = ctx.enter_context(tc.psum_pool(name="psum", bufs=1))

        def zeroed(name, shape):
            plane = keep.tile(shape, U8, name=name, align_bytes=64)
            nc.vector.memset(plane[:].bitcast(I32), 0)
            return plane

        def scale_rows(scales, experts):
            return scales[experts.start : experts.stop].rearrange("e s q n -> (e s) q n")

        def entries(lists, first, count):
            return lists[:, first // 16 : (first + count) // 16]

        def behind_product(e, shape, dtype, name, at):
            if e is None or e >= E:
                return keep.tile(shape, dtype, name=name, align_bytes=64)
            return shared.tile(shape, dtype, name=name, align_bytes=64, offset=W3_AT + e * FIRST_BYTES + at)

        x_plane = zeroed("x_plane", [P, T])
        early = [zeroed("early%d" % m, [P, len(EARLY) * PASSES, H]) for m in range(2)]
        moved = zeroed("moved", [P, E * C])
        late = {}
        identity = keep.tile([P, P], F32, name="identity")
        nc.vector.memset(identity[:], 0.0)
        make_identity(nc, identity[:], nomemset=True)

        first_words, second_words = {}, {}

        def load_first(e, m):
            at = (W1_AT, W3_AT)[m] + e * FIRST_BYTES
            name = "w%d_%d" % (2 * m + 1, e)
            first_words[e, m] = shared.tile([P, PASSES, 2 * H], U8, name=name, align_bytes=64, offset=at)
            rows = (w1_words, w3_words)[m][e].rearrange("s p b -> p s b")
            nc.sync.dma_start(out=first_words[e, m][:].bitcast(I32), in_=rows.bitcast(I32))

        offs_sb = keep.tile([P, T // 16], U16, name="offs_sb")
        nc.sync.dma_start(offs_sb[:], offs)
        load_first(0, 0)
        gate_row = keep.tile([P, GATE_ROW], F32, name="gate_row")
        nc.sync.dma_start(out=gate_row[:], in_=gate[0].rearrange("(p j) -> p j", j=GATE_ROW))
        x_rows = x_scales.rearrange("s (q r) t -> r q s t", r=4)
        for r in range(4):
            nc.sync.dma_start(out=x_plane[r:P:16, :].bitcast(I32), in_=x_rows[r].bitcast(I32))
        x_sb = shared.tile([P, PASSES, T], I32, name="x_sb", align_bytes=64, offset=X_AT)
        nc.sync.dma_start(out=x_sb[:], in_=x_words.rearrange("s p t r -> p s (t r)").bitcast(I32))
        for m in range(2):
            load_scale_rows(nc.sync, early[m], scale_rows((w1_scales, w3_scales)[m], EARLY))

        both = keep.tile([P, E * C], U8, name="both", align_bytes=64)
        for first in range(0, E * C, T // 2):
            nc.vector.tensor_copy(both[:, first : first + T // 2], x_plane[:].indirect(entries(offs_sb, first, T // 2)))


        def load_late_rows(m):
            at = X_AT + m * T * 4
            late[m] = shared.tile([P, len(LATE) * PASSES, H], U8, name="late%d" % m, align_bytes=64, offset=at)
            load_scale_rows(nc.sync, late[m], scale_rows((w1_scales, w3_scales)[m], LATE))

        def load_second(experts):
            tile = keep.tile([P, len(experts), 2 * N], U8, name="w2_%d" % experts.start, align_bytes=64)
            rows = w2_words.bitcast(I32)[experts.start : experts.stop].rearrange("e s p b -> p (e s) b")
            nc.sync.dma_start(out=tile[:].bitcast(I32), in_=rows)
            for i, e in enumerate(experts):
                second_words[e] = tile[:, i, :]

        for r in range(4):
            nc.sync.dma_start(out=moved[r:P:32, :].bitcast(I32), in_=both[16 + r : P : 32, :].bitcast(I32))
        load_first(0, 1)
        for m in range(2):
            load_first(1, m)
        for m in range(2):
            load_first(2, m)
        load_first(3, 0)

        slot_words = {}

        def gather_words(experts, s, behind):
            name = "words%d_%d" % (experts.start, s)
            words = behind_product(behind, [P, len(experts) * C], U32, name, 0)
            offsets = entries(offs_sb, experts.start * C, len(experts) * C)
            nc.vector.tensor_copy(words[:], x_sb[:, s, :].bitcast(U32).indirect(offsets))
            for i, e in enumerate(experts):
                slot_words[e, s] = words[:, i * C : (i + 1) * C]

        for experts in WORD_GATHERS[:-1]:
            for s in range(PASSES):
                gather_words(experts, s, None)
        gather_words(WORD_GATHERS[-1], 0, None)

        gate_sb = keep.tile([P, E * C], F32, name="gate_sb")
        for u in range(GATE_ROW // 4):
            spread = psum.tile([P, 4, P], F32, name="spread", tag="y%d" % u)
            for j in range(4):
                column = gate_row[:, 4 * u + j : 4 * u + j + 1].to_broadcast([P, P])
                nc.tensor.transpose(spread[:, j, :], column, identity[:])
            nc.scalar.copy(
                gate_sb[:].rearrange("m (p j) -> m p j", j=GATE_ROW)[:, :, 4 * u : 4 * u + 4],
                spread[:].rearrange("m j p -> m p j"),
            )

        banks, rectified, hidden, grouped, quantised, results, staged = {}, {}, {}, {}, {}, {}, {}
        windows = [keep.tile([P, T], F32, name="window%d" % half) for half in range(HALVES)]

        def woven(bank):
            return bank[:].rearrange("c (p u v) -> c u p v", u=2, v=2)

        def split(tile):
            return tile[:].rearrange("c (u p v) -> c u p v", u=2, v=2)

        def first_layer(e, m):
            bank = psum.tile([P, H], F32, name="sums", tag="a" if m == 0 else "b%d" % (e % 2))
            plane, first = (early[m], EARLY.start) if e in EARLY else (late[m], LATE.start)
            for s in range(PASSES):
                nc.tensor.matmul_mx(
                    out=bank[:],
                    lhsT=slot_words[e, s].bitcast(FP8X4),
                    lhsT_scale=(both, moved)[s][:, e * C : (e + 1) * C],
                    rhs=first_words[e, m][:, s, :].bitcast(FP4X4),
                    rhs_scale=plane[:, (e - first) * PASSES + s, :],
                    start=(s == 0),
                    stop=(s == PASSES - 1),
                )
            banks[e, m] = bank

        def rectify(e):
            first_layer(e, 0)
            rectified[e] = work.tile([P, H], F32, name="relu", align_bytes=64)
            nc.scalar.activation(split(rectified[e]), woven(banks[e, 0]), RELU)

        def product(e):
            hidden[e] = work.tile([P, H], BF16, name="h", align_bytes=64)
            nc.vector.tensor_tensor(split(hidden[e]), woven(banks[e, 1]), split(rectified[e]), MULT)

        def turn(e):
            turned = psum.tile([P, 2, C], F32, name="turned", tag="turn%d" % (e % 2))
            pairs = hidden[e][:].bitcast(F32)
            for u in range(2):
                nc.tensor.transpose(turned[:, u, :], pairs[:, u * P : (u + 1) * P], identity[:])
            grouped[e] = work.tile([P, C * 4], BF16, name="grouped", align_bytes=64)
            nc.scalar.copy(
                grouped[e][:].bitcast(F32).rearrange("p (c u) -> p c u", u=2), turned[:].rearrange("p u c -> p c u")
            )

        def quantise(e, behind):
            codes = behind_product(behind, [P, C], U32, "codes%d" % e, CODES_AT)
            plane = keep.tile([P, C], U8, name="h_plane%d" % e, align_bytes=64)
            nc.vector.quantize_mx(out=codes[:].bitcast(FP8X4), scales=plane[:], in_=grouped[e][:])
            quantised[e] = (codes, plane)

        def second_layer(e):
            codes, plane = quantised[e]
            results[e] = psum.tile([P, HALVES, C], F32, name="y_bank", tag="y%d" % (e % 2))
            for half in range(HALVES):
                nc.tensor.matmul_mx(
                    out=results[e][:, half, :],
                    lhsT=second_words[e][:, half * 2 * P : (half + 1) * 2 * P].bitcast(FP4X4),
                    lhsT_scale=w2_plane[:, e, half * P : (half + 1) * P],
                    rhs=codes[:].bitcast(FP8X4),
                    rhs_scale=plane[:],
                    start=True,
                    stop=True,
                )

        def weigh(e, behind):
            staged[e] = behind_product(behind, [P, HALVES, C], F32, "staged%d" % e, STAGED_AT)
            weights = gate_sb[:, e * C : (e + 1) * C].unsqueeze(1).to_broadcast([P, HALVES, C])
            nc.vector.tensor_tensor(staged[e][:], results[e][:], weights, MULT)

        def scatter(e):
            offsets = entries(dst_sb, e * C, C)
            for half in range(HALVES):
                if VECTOR_HALF.get(e) == half:
                    nc.vector.tensor_copy(windows[half][:].indirect(offsets), staged[e][:, half, :])
                else:
                    nc.scalar.activation(windows[half][:].indirect(offsets), staged[e][:, half, :], COPY)

        rectify(0)
        w2_plane = shared.tile([P, E, N], U8, name="w2_plane", align_bytes=64, offset=W1_AT)
        load_scale_rows(nc.sync, w2_plane, scale_rows(w2_scales, range(E)))
        load_second(range(0, 2))
        dst_sb = keep.tile([P, T // 16], U16, name="dst_sb")
        nc.sync.dma_start(dst_sb[:], dst)
        first_layer(0, 1)
        rectify(1)
        for step in range(E - 1):
            product(step)
            turn(step)
            if step + 1 < E:
                first_layer(step + 1, 1)
            if step == 1:
                load_late_rows(0)
                load_first(3, 1)
                load_first(4, 0)
                load_late_rows(1)
                load_second(range(2, 5))
                for e in LATE:
                    load_first(e, 1)
                    if e + 1 < E:
                        load_first(e + 1, 0)
                load_second(range(5, 8))
                weigh(0, None)
                scatter(0)
            if step >= 3:
                weigh(step - 2, step)
            if step >= 2:
                quantise(step - 1, step)
            if step >= 3:
                scatter(step - 2)
            if step == 0:
                gather_words(WORD_GATHERS[-1], 1, 0)
                quantise(0, None)
                second_layer(0)
            if step >= 2:
                second_layer(step - 1)
            if step + 2 < E:
                rectify(step + 2)
        last = E - 1
        weigh(last - 2, None)
        product(last)
        turn(last)
        quantise(last - 1, last)
        second_layer(last - 1)
        scatter(last - 2)
        weigh(last - 1, None)
        quantise(last, None)
        second_layer(last)
        scatter(last - 1)
        weigh(last, None)
        scatter(last)
        for half in range(HALVES):
            nc.sync.dma_start(out=out[half * P : (half + 1) * P, :], in_=windows[half][:])
